import numpy as np
import ml_dtypes


def mxq(x, axis, fmt="e4m3"):
    dtype, down = {"e4m3": (ml_dtypes.float8_e4m3fn, 7), "e5m2": (ml_dtypes.float8_e5m2, 14)}[fmt]
    v = np.moveaxis(np.asarray(x, np.float32).astype(ml_dtypes.bfloat16).astype(np.float64), axis, -1)
    blocks = v.reshape(v.shape[:-1] + (-1, 32))
    amax = np.abs(blocks).max(-1, keepdims=True)
    byte = np.maximum(np.where(amax > 0, np.frexp(amax)[1] - 1 + 127, 0) - down, 1)
    scale = np.exp2(byte - 127.0)
    codes = (blocks / scale).astype(np.float32).astype(dtype).astype(np.float64)
    return np.moveaxis((codes * scale).reshape(v.shape), -1, axis)


WIDE = False


def mx_kscale(k):
    if not WIDE:
        return np.ones(k)
    levels = np.array([10, -10, 5, -5, 0])
    if k % 512:
        return np.exp2(np.random.permutation(np.resize(levels, k // 32))).repeat(32)
    a = np.empty((k // 512, 16))
    for p in range(k // 512):
        a[p, :8] = np.random.permutation(np.resize(levels, 8))
        for g in range(8):
            far = levels[np.abs(levels - a[p, g]) >= 10]
            a[p, g + 8] = far[np.random.randint(len(far))]
    return np.exp2(a.ravel()).repeat(32)


def f64(x):
    return np.asarray(x).astype(np.float64)


def striped(idx):
    return np.tile(np.asarray(idx).reshape(-1, 16).T, (8, 1)).astype(np.uint16)


def unstriped(offs):
    return offs[:16].T.reshape(-1).astype(np.int64)


E2M1 = np.array([0.0, 0.5, 1.0, 1.5, 2.0, 3.0, 4.0, 6.0, -0.0, -0.5, -1.0, -1.5, -2.0, -3.0, -4.0, -6.0])


def pack_weight(w, fmt):
    k, n = w.shape
    w = f64(np.asarray(w, np.float32).astype(ml_dtypes.bfloat16)).reshape(k // 32, 32, n)
    amax = np.abs(w).max(1)
    if fmt == "e4m3":
        byte = np.frexp(amax)[1] - 1 + 127 - 7
    else:
        mant, ex = np.frexp(amax / 6.0)
        byte = np.where(mant > 0.5, ex, ex - 1) + 127
    byte = np.clip(np.where(amax > 0, byte, 1), 1, 254)
    scaled = (w * np.exp2(127.0 - byte)[:, None, :]).reshape(k, n).astype(np.float32)
    by_word = np.ascontiguousarray(scaled.reshape(k // 512, 128, 4, n).transpose(0, 1, 3, 2))
    if fmt == "e4m3":
        words = by_word.astype(ml_dtypes.float8_e4m3fn).view(np.uint8)
    else:
        c = by_word.astype(ml_dtypes.float4_e2m1fn).view(np.uint8) & 0xF
        words = (c[..., 0::2] | (c[..., 1::2] << 4)).reshape(k // 512, 128, 2 * n)
    return np.ascontiguousarray(words), np.ascontiguousarray(byte.astype(np.uint8).reshape(k // 512, 16, n))


def unpack_weight(words, scales, fmt):
    g, _, n = scales.shape
    words = np.ascontiguousarray(words).reshape(g, 128, n, -1)
    if fmt == "e4m3":
        vals = words.view(ml_dtypes.float8_e4m3fn).astype(np.float64)
    else:
        nib = np.empty((g, 128, n, 4), np.uint8)
        nib[..., 0::2] = words & 0xF
        nib[..., 1::2] = words >> 4
        vals = E2M1[nib]
    vals = vals * np.repeat(np.exp2(scales.astype(np.float64) - 127.0), 8, axis=1)[..., None]
    return vals.transpose(0, 1, 3, 2).reshape(g * 512, n)


B, N, T, D, DV, NQ = 1, 1024, 4096, 512, 256, 128
PAGE = 512


def setup_inputs():
    n = np.random.standard_normal
    pages = np.random.permutation(T // PAGE)[:B * N // PAGE]
    idx = (pages[:, None] * PAGE + np.arange(PAGE)[None, :]).reshape(-1)
    s = mx_kscale(D)[:, None]
    u = np.ones(T)
    u[idx] = mx_kscale(B * N)
    r = np.random.uniform(0.5, 2.0, T)
    k = n((D, T)) / s
    v = n((DV, T)) / (u * r)
    kp = pack_weight(k, "e4m3")
    vp = pack_weight(v.T, "e4m3")
    return {
        "qT": (n((B, D, NQ)) * s * (1.00 / np.sqrt(D))).astype(np.float32),
        "k_words": kp[0],
        "k_scales": kp[1],
        "v_words": vp[0],
        "v_scales": vp[1],
        "vs": np.tile(u * r, (128, 1)).astype(np.float32),
        "offs": striped(idx),
        "voffs": striped((pages[:, None] * DV + np.arange(DV)[None, :]).reshape(-1)),
    }


def reference(qT, k_words, k_scales, v_words, v_scales, vs, offs, voffs):
    idx = unstriped(offs)
    k = unpack_weight(k_words, k_scales, "e4m3")
    v = unpack_weight(v_words, v_scales, "e4m3")
    v = v.reshape(T // 512, 512, DV)[unstriped(voffs)[::DV] // DV].reshape(B, N, DV)
    pick = lambda x: x[:, idx].reshape(x.shape[0], B, N).transpose(1, 0, 2)
    q = f64(qT)
    score = mxq(q, 1, "e4m3").transpose(0, 2, 1) @ pick(k)
    m = score.max(-1, keepdims=True)
    p = np.exp(score - m)
    total = p.sum(-1, keepdims=True)
    w = p * pick(f64(vs))[:, :1, :]
    y = mxq(w, 2, "e4m3") @ v
    y = y / total
    return y

@@ -1,0 +1,180 @@
+from contextlib import ExitStack
+
+import concourse.mybir as mybir
+from concourse.masks import make_identity
+
+F32 = mybir.dt.float32
+BF16 = mybir.dt.bfloat16
+I32 = mybir.dt.int32
+U32 = mybir.dt.uint32
+U16 = mybir.dt.uint16
+U8 = mybir.dt.uint8
+FP8X4 = mybir.dt.float8_e4m3fn_x4
+ALU = mybir.AluOpType
+ACT = mybir.ActivationFunctionType
+AX = mybir.AxisListType
+
+P = 128
+PACK = 4
+PAGE = 512
+N, T, D, DV, NQ = 1024, 4096, 512, 256, 128
+PAGES = N // PAGE
+POOL_PAGES = T // PAGE
+V_ROW0 = 4
+VS_ROW = P - 1
+HALF = DV // 2
+
+FLOPS = 2 * NQ * N * (D + DV)
+
+
+def tile_attend_pkv8_soft_kernel(tc, qT, k_words, k_scales, v_words, v_scales, vs, offs, voffs, out):
+    nc = tc.nc
+    with ExitStack() as ctx:
+        lists = ctx.enter_context(tc.tile_pool(name="lists", bufs=1))
+        sb = ctx.enter_context(tc.tile_pool(name="sb", bufs=1))
+        ps = ctx.enter_context(tc.psum_pool(name="ps", bufs=1))
+
+        off_t = lists.tile([P, N // 16], U16, name="off_t")
+        voff_t = lists.tile([P, PAGES * DV // 16], U16, name="voff_t")
+        q_raw = sb.tile([P, PACK, NQ], F32, name="q_raw")
+        k_pool = sb.tile([P, T], I32, name="k_pool", align_bytes=64)
+        v_pool = sb.tile([P, POOL_PAGES * DV], I32, name="v_pool", align_bytes=64)
+        ks_pool = sb.tile([P, T], U8, name="ks_pool", tag="ks_then_keys", align_bytes=64)
+        vsc_pool = sb.tile([P, POOL_PAGES * DV], U8, name="vsc_pool", align_bytes=64)
+        tok_pool = sb.tile([P, T], F32, name="tok_pool", tag="tok_then_ks", align_bytes=64)
+
+        nc.vector.memset(ks_pool[:].bitcast(I32), 0)
+        nc.vector.memset(vsc_pool[:].bitcast(I32), 0)
+        warm = sb.tile([P, 1], F32, name="warm")
+        nc.vector.memset(warm[:], 0.0)
+        nc.vector.memset(tok_pool[0:VS_ROW, :], 0.0)
+
+        nc.sync.dma_start(off_t[:], offs)
+        nc.scalar.dma_start(q_raw[:], qT[0].rearrange("(p j) q -> p j q", j=PACK))
+        nc.sync.dma_start(k_pool[:], k_words[0].rearrange("p n t -> p (n t)").bitcast(I32))
+        nc.scalar.dma_start(tok_pool[VS_ROW:P, :], vs[0:1, :])
+        ks_rows = k_scales[0].bitcast(I32).rearrange("(a r) n -> r a n", r=4)
+        for r in range(4):
+            nc.scalar.dma_start(ks_pool[:].bitcast(I32)[r:P:32, :], ks_rows[r])
+        nc.sync.dma_start(voff_t[:], voffs)
+        nc.sync.dma_start(
+            v_pool[:].rearrange("p (u e) -> p u e", e=DV),
+            v_words.rearrange("u p e t -> p u (e t)").bitcast(I32),
+        )
+        ident = sb.tile([P, P], F32, name="ident")
+        make_identity(nc, ident[:])
+        vsc_rows = v_scales.bitcast(I32).rearrange("u (a r) e -> r a u e", r=4)
+        for r in range(4):
+            nc.gpsimd.dma_start(
+                vsc_pool[:].bitcast(I32)[V_ROW0 + r : P : 32, :].rearrange("p (u e) -> p u e", u=POOL_PAGES),
+                vsc_rows[r],
+            )
+
+        warm_out = sb.tile([P, 1], F32, name="warm_out")
+        nc.scalar.activation(warm_out[:], warm[:], ACT.Exp)
+
+        q_bf = sb.tile([P, NQ, PACK], BF16, name="q_bf", align_bytes=64)
+        nc.scalar.copy(q_bf[:], q_raw[:].rearrange("p j q -> p q j"))
+        q_codes = sb.tile([P, NQ], U32, name="q_codes", align_bytes=64)
+        q_sc = sb.tile([P, NQ], U8, name="q_sc", align_bytes=64)
+        nc.vector.quantize_mx(out=q_codes[:].bitcast(FP8X4), scales=q_sc[:], in_=q_bf[:].rearrange("p q j -> p (q j)"))
+
+        tok_g = sb.tile([P, N], F32, name="tok_g")
+        nc.vector.tensor_copy(tok_g[:], tok_pool[:].indirect(off_t[:]))
+        tok_col = sb.tile([P, PAGES, PACK], F32, name="tok_col")
+        for g in range(PAGES):
+            tok_ps = ps.tile([P, PACK, P], F32, name=f"tok_ps{g}")
+            for t in range(PACK):
+                nc.tensor.transpose(tok_ps[:, t, :], tok_g[:, g * PAGE + t : (g + 1) * PAGE : PACK], ident[:])
+            nc.scalar.copy(tok_col[:, g, :], tok_ps[:, :, VS_ROW])
+
+        ks_g = sb.tile([P, N], U8, name="ks_g", tag="tok_then_ks", align_bytes=64)
+        nc.vector.tensor_copy(ks_g[:], ks_pool[:].indirect(off_t[:]))
+
+        k_g = sb.tile([P, N], U32, name="k_g", tag="ks_then_keys", align_bytes=64)
+        scores = []
+        for g in range(PAGES):
+            cols = slice(g * PAGE, (g + 1) * PAGE)
+            nc.vector.tensor_copy(
+                k_g[:, cols], k_pool[:].bitcast(U32).indirect(off_t[:, g * PAGE // 16 : (g + 1) * PAGE // 16])
+            )
+            score = ps.tile([NQ, PAGE], F32, name=f"score{g}")
+            nc.tensor.matmul_mx(
+                out=score[:],
+                lhsT=q_codes[:].bitcast(FP8X4),
+                lhsT_scale=q_sc[:],
+                rhs=k_g[:, cols].bitcast(FP8X4),
+                rhs_scale=ks_g[:, cols],
+                start=True,
+                stop=True,
+            )
+            scores.append(score)
+
+        page_max = []
+        for g in range(PAGES):
+            mx = sb.tile([NQ, 1], F32, name=f"mx{g}", tag=f"max_then_v{g}", align_bytes=64)
+            nc.vector.tensor_reduce(mx[:], scores[g][:], AX.X, ALU.max)
+            page_max.append(mx)
+        neg_max = sb.tile([NQ, 1], F32, name="neg_max")
+        nc.vector.tensor_scalar(neg_max[:], page_max[0][:], page_max[1][:], -1.0, ALU.max, ALU.mult)
+
+        v_g = sb.tile([P, PAGES * DV], U32, name="v_g", tag="max_then_v0", align_bytes=64)
+        nc.vector.tensor_copy(v_g[:], v_pool[:].bitcast(U32).indirect(voff_t[:]))
+        vsc_g = sb.tile([P, PAGES * DV], U8, name="vsc_g", tag="max_then_v1", align_bytes=64)
+        nc.vector.tensor_copy(vsc_g[:], vsc_pool[:].indirect(voff_t[:]))
+
+        page_sum = sb.tile([NQ, PAGES], F32, name="page_sum")
+        w_bf = []
+        for g in range(PAGES):
+            prob = sb.tile([NQ, PACK, P], F32, name=f"prob{g}")
+            nc.scalar.activation(
+                prob[:],
+                scores[g][:].rearrange("q (s t) -> q t s", t=PACK),
+                ACT.Exp,
+                bias=neg_max[:],
+                scale=1.0,
+                accum_out=page_sum[:, g : g + 1],
+            )
+            prob_t = ps.tile([P, PACK, NQ], F32, name=f"prob_t{g}")
+            for t in range(PACK):
+                nc.tensor.transpose(prob_t[:, t, :], prob[:, t, :], ident[:])
+            w = sb.tile([P, NQ, PACK], BF16, name=f"w{g}", align_bytes=64)
+            nc.vector.tensor_tensor(
+                w[:],
+                prob_t[:].rearrange("s t q -> s q t"),
+                tok_col[:, g, :].unsqueeze(1).to_broadcast([P, NQ, PACK]),
+                ALU.mult,
+            )
+            w_bf.append(w)
+
+        total = sb.tile([NQ, 1], F32, name="total")
+        nc.scalar.activation(total[:], page_sum[:, 0:1], ACT.Identity, bias=page_sum[:, 1:2], scale=1.0)
+        inv_total = sb.tile([NQ, 1], F32, name="inv_total")
+
+        acc = [ps.tile([NQ, HALF], F32, name=f"acc{h}") for h in range(2)]
+        for g in range(PAGES):
+            w_codes = sb.tile([P, NQ], U32, name=f"w_codes{g}", align_bytes=64)
+            w_sc = sb.tile([P, NQ], U8, name=f"w_sc{g}", align_bytes=64)
+            nc.vector.quantize_mx(
+                out=w_codes[:].bitcast(FP8X4), scales=w_sc[:], in_=w_bf[g][:].rearrange("s q t -> s (q t)")
+            )
+            if g == 0:
+                nc.vector.reciprocal(inv_total[:], total[:])
+            for h in range(2):
+                cols = slice(g * DV + h * HALF, g * DV + (h + 1) * HALF)
+                nc.tensor.matmul_mx(
+                    out=acc[h][:],
+                    lhsT=w_codes[:].bitcast(FP8X4),
+                    lhsT_scale=w_sc[:],
+                    rhs=v_g[:, cols].bitcast(FP8X4),
+                    rhs_scale=vsc_g[V_ROW0:P, cols],
+                    start=(g == 0),
+                    stop=(g == PAGES - 1),
+                )
+
+        y0 = sb.tile([NQ, HALF], F32, name="y0")
+        nc.vector.tensor_scalar(y0[:], acc[0][:], inv_total[:], None, ALU.mult)
+        nc.sync.dma_start(out[0][:, 0:HALF], y0[:])
+        y1 = sb.tile([NQ, HALF], F32, name="y1")
+        nc.scalar.activation(y1[:], acc[1][:], ACT.Copy, scale=inv_total[:])
+        nc.scalar.dma_start(out[0][:, HALF:DV], y1[:])

@@ -23,6 +23,7 @@ POOL_PAGES = T // PAGE
 V_ROW0 = 4
 VS_ROW = P - 1
 HALF = DV // 2
+PART = PAGE // 2
 
 FLOPS = 2 * NQ * N * (D + DV)
 
@@ -36,54 +37,54 @@ def tile_attend_pkv8_soft_kernel(tc, qT, k_words, k_scales, v_words, v_scales, v
 
         off_t = lists.tile([P, N // 16], U16, name="off_t")
         voff_t = lists.tile([P, PAGES * DV // 16], U16, name="voff_t")
-        q_raw = sb.tile([P, PACK, NQ], F32, name="q_raw")
+        q_raw = sb.tile([P, PACK, NQ], F32, name="q_raw", tag="q_then_v", align_bytes=64)
         k_pool = sb.tile([P, T], I32, name="k_pool", align_bytes=64)
-        v_pool = sb.tile([P, POOL_PAGES * DV], I32, name="v_pool", align_bytes=64)
         ks_pool = sb.tile([P, T], U8, name="ks_pool", tag="ks_then_keys", align_bytes=64)
-        vsc_pool = sb.tile([P, POOL_PAGES * DV], U8, name="vsc_pool", align_bytes=64)
+        vsc_pool = sb.tile([P, POOL_PAGES * DV], U8, name="vsc_pool", tag="vsc_then_v", align_bytes=64)
         tok_pool = sb.tile([P, T], F32, name="tok_pool", tag="tok_then_ks", align_bytes=64)
 
         nc.vector.memset(ks_pool[:].bitcast(I32), 0)
-        nc.vector.memset(vsc_pool[:].bitcast(I32), 0)
         warm = sb.tile([P, 1], F32, name="warm")
         nc.vector.memset(warm[:], 0.0)
         nc.vector.memset(tok_pool[0:VS_ROW, :], 0.0)
+        nc.vector.memset(vsc_pool[:].bitcast(I32), 0)
 
         nc.sync.dma_start(off_t[:], offs)
         nc.scalar.dma_start(q_raw[:], qT[0].rearrange("(p j) q -> p j q", j=PACK))
-        nc.sync.dma_start(k_pool[:], k_words[0].rearrange("p n t -> p (n t)").bitcast(I32))
+        nc.sync.dma_start(voff_t[:], voffs)
         nc.scalar.dma_start(tok_pool[VS_ROW:P, :], vs[0:1, :])
+        nc.sync.dma_start(k_pool[:], k_words[0].rearrange("p n t -> p (n t)").bitcast(I32))
         ks_rows = k_scales[0].bitcast(I32).rearrange("(a r) n -> r a n", r=4)
         for r in range(4):
             nc.scalar.dma_start(ks_pool[:].bitcast(I32)[r:P:32, :], ks_rows[r])
-        nc.sync.dma_start(voff_t[:], voffs)
-        nc.sync.dma_start(
-            v_pool[:].rearrange("p (u e) -> p u e", e=DV),
-            v_words.rearrange("u p e t -> p u (e t)").bitcast(I32),
-        )
         ident = sb.tile([P, P], F32, name="ident")
         make_identity(nc, ident[:])
-        vsc_rows = v_scales.bitcast(I32).rearrange("u (a r) e -> r a u e", r=4)
-        for r in range(4):
-            nc.gpsimd.dma_start(
-                vsc_pool[:].bitcast(I32)[V_ROW0 + r : P : 32, :].rearrange("p (u e) -> p u e", u=POOL_PAGES),
-                vsc_rows[r],
-            )
 
         warm_out = sb.tile([P, 1], F32, name="warm_out")
         nc.scalar.activation(warm_out[:], warm[:], ACT.Exp)
 
         q_bf = sb.tile([P, NQ, PACK], BF16, name="q_bf", align_bytes=64)
         nc.scalar.copy(q_bf[:], q_raw[:].rearrange("p j q -> p q j"))
+        v_pool = sb.tile([P, POOL_PAGES * DV], I32, name="v_pool", tag="q_then_v", align_bytes=64)
+        nc.sync.dma_start(
+            v_pool[:].rearrange("p (u e) -> p u e", e=DV),
+            v_words.rearrange("u p e t -> p u (e t)").bitcast(I32),
+        )
+        vsc_rows = v_scales.bitcast(I32).rearrange("u (a r) e -> r a u e", r=4)
+        for r in range(4):
+            nc.sync.dma_start(
+                vsc_pool[:].bitcast(I32)[V_ROW0 + r : P : 32, :].rearrange("p (u e) -> p u e", u=POOL_PAGES),
+                vsc_rows[r],
+            )
         q_codes = sb.tile([P, NQ], U32, name="q_codes", align_bytes=64)
         q_sc = sb.tile([P, NQ], U8, name="q_sc", align_bytes=64)
         nc.vector.quantize_mx(out=q_codes[:].bitcast(FP8X4), scales=q_sc[:], in_=q_bf[:].rearrange("p q j -> p (q j)"))
 
         tok_g = sb.tile([P, N], F32, name="tok_g")
         nc.vector.tensor_copy(tok_g[:], tok_pool[:].indirect(off_t[:]))
-        tok_col = sb.tile([P, PAGES, PACK], F32, name="tok_col")
+        tok_col = sb.tile([P, PAGES, PACK], F32, name="tok_col", tag="tok_then_codes", align_bytes=64)
         for g in range(PAGES):
-            tok_ps = ps.tile([P, PACK, P], F32, name=f"tok_ps{g}")
+            tok_ps = ps.tile([P, PACK, P], F32, name=f"tok_ps{g}", tag=f"turned{g}")
             for t in range(PACK):
                 nc.tensor.transpose(tok_ps[:, t, :], tok_g[:, g * PAGE + t : (g + 1) * PAGE : PACK], ident[:])
             nc.scalar.copy(tok_col[:, g, :], tok_ps[:, :, VS_ROW])
@@ -98,44 +99,46 @@ def tile_attend_pkv8_soft_kernel(tc, qT, k_words, k_scales, v_words, v_scales, v
             nc.vector.tensor_copy(
                 k_g[:, cols], k_pool[:].bitcast(U32).indirect(off_t[:, g * PAGE // 16 : (g + 1) * PAGE // 16])
             )
-            score = ps.tile([NQ, PAGE], F32, name=f"score{g}")
-            nc.tensor.matmul_mx(
-                out=score[:],
-                lhsT=q_codes[:].bitcast(FP8X4),
-                lhsT_scale=q_sc[:],
-                rhs=k_g[:, cols].bitcast(FP8X4),
-                rhs_scale=ks_g[:, cols],
-                start=True,
-                stop=True,
-            )
-            scores.append(score)
+            for h in range(2):
+                part = slice(g * PAGE + h * PART, g * PAGE + (h + 1) * PART)
+                score = ps.tile([NQ, PART], F32, name=f"score{g}{h}")
+                nc.tensor.matmul_mx(
+                    out=score[:],
+                    lhsT=q_codes[:].bitcast(FP8X4),
+                    lhsT_scale=q_sc[:],
+                    rhs=k_g[:, part].bitcast(FP8X4),
+                    rhs_scale=ks_g[:, part],
+                    start=True,
+                    stop=True,
+                )
+                scores.append(score)
 
-        page_max = []
-        for g in range(PAGES):
-            mx = sb.tile([NQ, 1], F32, name=f"mx{g}", tag=f"max_then_v{g}", align_bytes=64)
-            nc.vector.tensor_reduce(mx[:], scores[g][:], AX.X, ALU.max)
-            page_max.append(mx)
+        part_max = sb.tile([NQ, 4], F32, name="part_max", tag="max_then_vsc", align_bytes=64)
+        for i in range(4):
+            nc.vector.tensor_reduce(part_max[:, i : i + 1], scores[i][:], AX.X, ALU.max)
         neg_max = sb.tile([NQ, 1], F32, name="neg_max")
-        nc.vector.tensor_scalar(neg_max[:], page_max[0][:], page_max[1][:], -1.0, ALU.max, ALU.mult)
+        nc.vector.tensor_reduce(neg_max[:], part_max[:], AX.X, ALU.max, negate=True)
 
-        v_g = sb.tile([P, PAGES * DV], U32, name="v_g", tag="max_then_v0", align_bytes=64)
-        nc.vector.tensor_copy(v_g[:], v_pool[:].bitcast(U32).indirect(voff_t[:]))
-        vsc_g = sb.tile([P, PAGES * DV], U8, name="vsc_g", tag="max_then_v1", align_bytes=64)
+        vsc_g = sb.tile([P, PAGES * DV], U8, name="vsc_g", tag="max_then_vsc", align_bytes=64)
         nc.vector.tensor_copy(vsc_g[:], vsc_pool[:].indirect(voff_t[:]))
+        v_g = sb.tile([P, PAGES * DV], U32, name="v_g", tag="vsc_then_v", align_bytes=64)
+        nc.vector.tensor_copy(v_g[:], v_pool[:].bitcast(U32).indirect(voff_t[:]))
 
-        page_sum = sb.tile([NQ, PAGES], F32, name="page_sum")
+        page_sum = sb.tile([NQ, 4], F32, name="page_sum")
         w_bf = []
         for g in range(PAGES):
             prob = sb.tile([NQ, PACK, P], F32, name=f"prob{g}")
-            nc.scalar.activation(
-                prob[:],
-                scores[g][:].rearrange("q (s t) -> q t s", t=PACK),
-                ACT.Exp,
-                bias=neg_max[:],
-                scale=1.0,
-                accum_out=page_sum[:, g : g + 1],
-            )
-            prob_t = ps.tile([P, PACK, NQ], F32, name=f"prob_t{g}")
+            for h in range(2):
+                i = 2 * g + h
+                nc.scalar.activation(
+                    prob[:, :, h * 64 : (h + 1) * 64],
+                    scores[i][:].rearrange("q (s t) -> q t s", t=PACK),
+                    ACT.Exp,
+                    bias=neg_max[:],
+                    scale=1.0,
+                    accum_out=page_sum[:, i : i + 1],
+                )
+            prob_t = ps.tile([P, PACK, NQ], F32, name=f"prob_t{g}", tag=f"turned{g}")
             for t in range(PACK):
                 nc.tensor.transpose(prob_t[:, t, :], prob[:, t, :], ident[:])
             w = sb.tile([P, NQ, PACK], BF16, name=f"w{g}", align_bytes=64)
@@ -148,12 +151,14 @@ def tile_attend_pkv8_soft_kernel(tc, qT, k_words, k_scales, v_words, v_scales, v
             w_bf.append(w)
 
         total = sb.tile([NQ, 1], F32, name="total")
-        nc.scalar.activation(total[:], page_sum[:, 0:1], ACT.Identity, bias=page_sum[:, 1:2], scale=1.0)
+        sum_copy = sb.tile([NQ, 4], F32, name="sum_copy")
+        nc.scalar.activation(sum_copy[:], page_sum[:], ACT.Identity, accum_out=total[:])
         inv_total = sb.tile([NQ, 1], F32, name="inv_total")
 
+        code_tags = ["tok_then_codes", "codes1"]
         acc = [ps.tile([NQ, HALF], F32, name=f"acc{h}") for h in range(2)]
         for g in range(PAGES):
-            w_codes = sb.tile([P, NQ], U32, name=f"w_codes{g}", align_bytes=64)
+            w_codes = sb.tile([P, NQ], U32, name=f"w_codes{g}", tag=code_tags[g], align_bytes=64)
             w_sc = sb.tile([P, NQ], U8, name=f"w_sc{g}", align_bytes=64)
             nc.vector.quantize_mx(
                 out=w_codes[:].bitcast(FP8X4), scales=w_sc[:], in_=w_bf[g][:].rearrange("s q t -> s (q t)")

@@ -72,7 +72,7 @@ def tile_attend_pkv8_soft_kernel(tc, qT, k_words, k_scales, v_words, v_scales, v
         )
         vsc_rows = v_scales.bitcast(I32).rearrange("u (a r) e -> r a u e", r=4)
         for r in range(4):
-            nc.sync.dma_start(
+            nc.scalar.dma_start(
                 vsc_pool[:].bitcast(I32)[V_ROW0 + r : P : 32, :].rearrange("p (u e) -> p u e", u=POOL_PAGES),
                 vsc_rows[r],
             )
@@ -131,8 +131,8 @@ def tile_attend_pkv8_soft_kernel(tc, qT, k_words, k_scales, v_words, v_scales, v
             for h in range(2):
                 i = 2 * g + h
                 nc.scalar.activation(
-                    prob[:, :, h * 64 : (h + 1) * 64],
-                    scores[i][:].rearrange("q (s t) -> q t s", t=PACK),
+                    prob[:, :, h * 64 : (h + 1) * 64].rearrange("q t s -> q s t"),
+                    scores[i][:].rearrange("q (s t) -> q s t", t=PACK),
                     ACT.Exp,
                     bias=neg_max[:],
                     scale=1.0,

@@ -72,7 +72,7 @@ def tile_attend_pkv8_soft_kernel(tc, qT, k_words, k_scales, v_words, v_scales, v
         )
         vsc_rows = v_scales.bitcast(I32).rearrange("u (a r) e -> r a u e", r=4)
         for r in range(4):
-            nc.scalar.dma_start(
+            nc.sync.dma_start(
                 vsc_pool[:].bitcast(I32)[V_ROW0 + r : P : 32, :].rearrange("p (u e) -> p u e", u=POOL_PAGES),
                 vsc_rows[r],
             )
@@ -82,12 +82,14 @@ def tile_attend_pkv8_soft_kernel(tc, qT, k_words, k_scales, v_words, v_scales, v
 
         tok_g = sb.tile([P, N], F32, name="tok_g")
         nc.vector.tensor_copy(tok_g[:], tok_pool[:].indirect(off_t[:]))
-        tok_col = sb.tile([P, PAGES, PACK], F32, name="tok_col", tag="tok_then_codes", align_bytes=64)
+        tok_cols = []
         for g in range(PAGES):
             tok_ps = ps.tile([P, PACK, P], F32, name=f"tok_ps{g}", tag=f"turned{g}")
             for t in range(PACK):
                 nc.tensor.transpose(tok_ps[:, t, :], tok_g[:, g * PAGE + t : (g + 1) * PAGE : PACK], ident[:])
-            nc.scalar.copy(tok_col[:, g, :], tok_ps[:, :, VS_ROW])
+            tok_col = sb.tile([P, PACK], F32, name=f"tok_col{g}", tag=f"tok_col{g}", align_bytes=64)
+            nc.scalar.copy(tok_col[:], tok_ps[:, :, VS_ROW])
+            tok_cols.append(tok_col)
 
         ks_g = sb.tile([P, N], U8, name="ks_g", tag="tok_then_ks", align_bytes=64)
         nc.vector.tensor_copy(ks_g[:], ks_pool[:].indirect(off_t[:]))
@@ -119,13 +121,13 @@ def tile_attend_pkv8_soft_kernel(tc, qT, k_words, k_scales, v_words, v_scales, v
         neg_max = sb.tile([NQ, 1], F32, name="neg_max")
         nc.vector.tensor_reduce(neg_max[:], part_max[:], AX.X, ALU.max, negate=True)
 
-        vsc_g = sb.tile([P, PAGES * DV], U8, name="vsc_g", tag="max_then_vsc", align_bytes=64)
-        nc.vector.tensor_copy(vsc_g[:], vsc_pool[:].indirect(voff_t[:]))
-        v_g = sb.tile([P, PAGES * DV], U32, name="v_g", tag="vsc_then_v", align_bytes=64)
+        v_g = sb.tile([P, PAGES * DV], U32, name="v_g", tag="max_then_vsc", align_bytes=64)
         nc.vector.tensor_copy(v_g[:], v_pool[:].bitcast(U32).indirect(voff_t[:]))
+        vsc_g = sb.tile([P, PAGES * DV], U8, name="vsc_g", tag="q_then_v", align_bytes=64)
+        nc.vector.tensor_copy(vsc_g[:], vsc_pool[:].indirect(voff_t[:]))
 
         page_sum = sb.tile([NQ, 4], F32, name="page_sum")
-        w_bf = []
+        w_bf = sb.tile([P, PAGES, NQ, PACK], BF16, name="w_bf", tag="vsc_then_v", align_bytes=64)
         for g in range(PAGES):
             prob = sb.tile([NQ, PACK, P], F32, name=f"prob{g}")
             for h in range(2):
@@ -141,27 +143,24 @@ def tile_attend_pkv8_soft_kernel(tc, qT, k_words, k_scales, v_words, v_scales, v
             prob_t = ps.tile([P, PACK, NQ], F32, name=f"prob_t{g}", tag=f"turned{g}")
             for t in range(PACK):
                 nc.tensor.transpose(prob_t[:, t, :], prob[:, t, :], ident[:])
-            w = sb.tile([P, NQ, PACK], BF16, name=f"w{g}", align_bytes=64)
             nc.vector.tensor_tensor(
-                w[:],
+                w_bf[:, g],
                 prob_t[:].rearrange("s t q -> s q t"),
-                tok_col[:, g, :].unsqueeze(1).to_broadcast([P, NQ, PACK]),
+                tok_cols[g][:].unsqueeze(1).to_broadcast([P, NQ, PACK]),
                 ALU.mult,
             )
-            w_bf.append(w)
 
         total = sb.tile([NQ, 1], F32, name="total")
         sum_copy = sb.tile([NQ, 4], F32, name="sum_copy")
         nc.scalar.activation(sum_copy[:], page_sum[:], ACT.Identity, accum_out=total[:])
-        inv_total = sb.tile([NQ, 1], F32, name="inv_total")
+        inv_total = sb.tile([NQ, 1], F32, name="inv_total", tag="tok_col0", align_bytes=64)
 
-        code_tags = ["tok_then_codes", "codes1"]
         acc = [ps.tile([NQ, HALF], F32, name=f"acc{h}") for h in range(2)]
         for g in range(PAGES):
-            w_codes = sb.tile([P, NQ], U32, name=f"w_codes{g}", tag=code_tags[g], align_bytes=64)
+            w_codes = sb.tile([P, NQ], U32, name=f"w_codes{g}", align_bytes=64)
             w_sc = sb.tile([P, NQ], U8, name=f"w_sc{g}", align_bytes=64)
             nc.vector.quantize_mx(
-                out=w_codes[:].bitcast(FP8X4), scales=w_sc[:], in_=w_bf[g][:].rearrange("s q t -> s (q t)")
+                out=w_codes[:].bitcast(FP8X4), scales=w_sc[:], in_=w_bf[:, g].rearrange("s q t -> s (q t)")
             )
             if g == 0:
                 nc.vector.reciprocal(inv_total[:], total[:])

@@ -38,7 +38,7 @@ def tile_attend_pkv8_soft_kernel(tc, qT, k_words, k_scales, v_words, v_scales, v
         off_t = lists.tile([P, N // 16], U16, name="off_t")
         voff_t = lists.tile([P, PAGES * DV // 16], U16, name="voff_t")
         q_raw = sb.tile([P, PACK, NQ], F32, name="q_raw", tag="q_then_v", align_bytes=64)
-        k_pool = sb.tile([P, T], I32, name="k_pool", align_bytes=64)
+        k_pool = sb.tile([P, T], I32, name="k_pool", tag="keys_then_warm", align_bytes=64)
         ks_pool = sb.tile([P, T], U8, name="ks_pool", tag="ks_then_keys", align_bytes=64)
         vsc_pool = sb.tile([P, POOL_PAGES * DV], U8, name="vsc_pool", tag="vsc_then_v", align_bytes=64)
         tok_pool = sb.tile([P, T], F32, name="tok_pool", tag="tok_then_ks", align_bytes=64)
@@ -115,6 +115,12 @@ def tile_attend_pkv8_soft_kernel(tc, qT, k_words, k_scales, v_words, v_scales, v
                 )
                 scores.append(score)
 
+        warm_src = sb.tile([P, P], F32, name="warm_src", tag="keys_then_warm", align_bytes=64)
+        nc.scalar.copy(warm_src[:], ident[:])
+        warm_ps = ps.tile([P, PACK, P], F32, name="warm_ps", tag="acc0")
+        for i in range(8):
+            nc.tensor.transpose(warm_ps[:, i % PACK, :], warm_src[:], ident[:])
+
         part_max = sb.tile([NQ, 4], F32, name="part_max", tag="max_then_vsc", align_bytes=64)
         for i in range(4):
             nc.vector.tensor_reduce(part_max[:, i : i + 1], scores[i][:], AX.X, ALU.max)
@@ -155,7 +161,7 @@ def tile_attend_pkv8_soft_kernel(tc, qT, k_words, k_scales, v_words, v_scales, v
         nc.scalar.activation(sum_copy[:], page_sum[:], ACT.Identity, accum_out=total[:])
         inv_total = sb.tile([NQ, 1], F32, name="inv_total", tag="tok_col0", align_bytes=64)
 
-        acc = [ps.tile([NQ, HALF], F32, name=f"acc{h}") for h in range(2)]
+        acc = [ps.tile([NQ, HALF], F32, name=f"acc{h}", tag=f"acc{h}") for h in range(2)]
         for g in range(PAGES):
             w_codes = sb.tile([P, NQ], U32, name=f"w_codes{g}", align_bytes=64)
             w_sc = sb.tile([P, NQ], U8, name=f"w_sc{g}", align_bytes=64)

@@ -1,7 +1,6 @@
 from contextlib import ExitStack
 
 import concourse.mybir as mybir
-from concourse.masks import make_identity
 
 F32 = mybir.dt.float32
 BF16 = mybir.dt.bfloat16
@@ -12,7 +11,6 @@ U8 = mybir.dt.uint8
 FP8X4 = mybir.dt.float8_e4m3fn_x4
 ALU = mybir.AluOpType
 ACT = mybir.ActivationFunctionType
-AX = mybir.AxisListType
 
 P = 128
 PACK = 4
@@ -23,7 +21,7 @@ POOL_PAGES = T // PAGE
 V_ROW0 = 4
 VS_ROW = P - 1
 HALF = DV // 2
-PART = PAGE // 2
+ZERO_SPLIT = 2560
 
 FLOPS = 2 * NQ * N * (D + DV)
 
@@ -37,118 +35,128 @@ def tile_attend_pkv8_soft_kernel(tc, qT, k_words, k_scales, v_words, v_scales, v
 
         off_t = lists.tile([P, N // 16], U16, name="off_t")
         voff_t = lists.tile([P, PAGES * DV // 16], U16, name="voff_t")
-        q_raw = sb.tile([P, PACK, NQ], F32, name="q_raw", tag="q_then_v", align_bytes=64)
-        k_pool = sb.tile([P, T], I32, name="k_pool", tag="keys_then_warm", align_bytes=64)
-        ks_pool = sb.tile([P, T], U8, name="ks_pool", tag="ks_then_keys", align_bytes=64)
-        vsc_pool = sb.tile([P, POOL_PAGES * DV], U8, name="vsc_pool", tag="vsc_then_v", align_bytes=64)
+        q_raw = sb.tile([P, PACK, NQ], F32, name="q_raw", align_bytes=64)
+        ks_pool = sb.tile([P, T], U8, name="ks_pool", align_bytes=64)
+        vsc_pool = sb.tile([P, POOL_PAGES * DV], U8, name="vsc_pool", align_bytes=64)
         tok_pool = sb.tile([P, T], F32, name="tok_pool", tag="tok_then_ks", align_bytes=64)
 
-        nc.vector.memset(ks_pool[:].bitcast(I32), 0)
-        warm = sb.tile([P, 1], F32, name="warm")
-        nc.vector.memset(warm[:], 0.0)
-        nc.vector.memset(tok_pool[0:VS_ROW, :], 0.0)
-        nc.vector.memset(vsc_pool[:].bitcast(I32), 0)
+        blank = sb.tile([P, P + 1], F32, name="blank", tag="blank_then_keys", align_bytes=64)
+        nc.vector.memset(blank[:], 0.0)
+        nc.gpsimd.memset(ks_pool[:].bitcast(I32), 0)
+        ident = sb.tile([P, P], F32, name="ident")
+        nc.gpsimd.affine_select(
+            out=ident[:],
+            in_=blank[:, 0:P],
+            compare_op=ALU.not_equal,
+            fill=1.0,
+            base=0,
+            pattern=[[-1, P]],
+            channel_multiplier=1,
+        )
+        nc.vector.memset(tok_pool[0:VS_ROW, 0 : ZERO_SPLIT - 1], 0.0)
+        nc.vector.memset(tok_pool[0:VS_ROW, ZERO_SPLIT - 1 : ZERO_SPLIT], 0.0)
+        nc.gpsimd.memset(tok_pool[0:VS_ROW, ZERO_SPLIT:T], 0.0)
+        nc.gpsimd.memset(vsc_pool[:].bitcast(I32), 0)
+        minus_one = sb.tile([NQ, 1], F32, name="minus_one")
+        nc.gpsimd.memset(minus_one[:], -1.0)
 
         nc.sync.dma_start(off_t[:], offs)
-        nc.scalar.dma_start(q_raw[:], qT[0].rearrange("(p j) q -> p j q", j=PACK))
-        nc.sync.dma_start(voff_t[:], voffs)
         nc.scalar.dma_start(tok_pool[VS_ROW:P, :], vs[0:1, :])
-        nc.sync.dma_start(k_pool[:], k_words[0].rearrange("p n t -> p (n t)").bitcast(I32))
+        nc.scalar.dma_start(q_raw[:], qT[0].rearrange("(p j) q -> p j q", j=PACK))
         ks_rows = k_scales[0].bitcast(I32).rearrange("(a r) n -> r a n", r=4)
         for r in range(4):
-            nc.scalar.dma_start(ks_pool[:].bitcast(I32)[r:P:32, :], ks_rows[r])
-        ident = sb.tile([P, P], F32, name="ident")
-        make_identity(nc, ident[:])
-
-        warm_out = sb.tile([P, 1], F32, name="warm_out")
-        nc.scalar.activation(warm_out[:], warm[:], ACT.Exp)
-
-        q_bf = sb.tile([P, NQ, PACK], BF16, name="q_bf", align_bytes=64)
-        nc.scalar.copy(q_bf[:], q_raw[:].rearrange("p j q -> p q j"))
-        v_pool = sb.tile([P, POOL_PAGES * DV], I32, name="v_pool", tag="q_then_v", align_bytes=64)
-        nc.sync.dma_start(
-            v_pool[:].rearrange("p (u e) -> p u e", e=DV),
-            v_words.rearrange("u p e t -> p u (e t)").bitcast(I32),
-        )
+            nc.sync.dma_start(ks_pool[:].bitcast(I32)[r:P:32, :], ks_rows[r])
+        k_pool = sb.tile([P, T], I32, name="k_pool", tag="blank_then_keys", align_bytes=64)
+        nc.sync.dma_start(k_pool[:], k_words[0].rearrange("p n t -> p (n t)").bitcast(I32))
+        nc.sync.dma_start(voff_t[:], voffs)
         vsc_rows = v_scales.bitcast(I32).rearrange("u (a r) e -> r a u e", r=4)
         for r in range(4):
             nc.sync.dma_start(
                 vsc_pool[:].bitcast(I32)[V_ROW0 + r : P : 32, :].rearrange("p (u e) -> p u e", u=POOL_PAGES),
                 vsc_rows[r],
             )
-        q_codes = sb.tile([P, NQ], U32, name="q_codes", align_bytes=64)
-        q_sc = sb.tile([P, NQ], U8, name="q_sc", align_bytes=64)
-        nc.vector.quantize_mx(out=q_codes[:].bitcast(FP8X4), scales=q_sc[:], in_=q_bf[:].rearrange("p q j -> p (q j)"))
+
+        q_bf = sb.tile([P, NQ, PACK], BF16, name="q_bf", tag="q_then_v", align_bytes=64)
+        nc.scalar.copy(q_bf[:], q_raw[:].rearrange("p j q -> p q j"))
 
         tok_g = sb.tile([P, N], F32, name="tok_g")
         nc.vector.tensor_copy(tok_g[:], tok_pool[:].indirect(off_t[:]))
         tok_cols = []
         for g in range(PAGES):
-            tok_ps = ps.tile([P, PACK, P], F32, name=f"tok_ps{g}", tag=f"turned{g}")
+            tok_ps = ps.tile([P, PACK, P], F32, name=f"tok_ps{g}")
             for t in range(PACK):
                 nc.tensor.transpose(tok_ps[:, t, :], tok_g[:, g * PAGE + t : (g + 1) * PAGE : PACK], ident[:])
-            tok_col = sb.tile([P, PACK], F32, name=f"tok_col{g}", tag=f"tok_col{g}", align_bytes=64)
+            tok_col = sb.tile([P, PACK], F32, name=f"tok_col{g}", align_bytes=64)
             nc.scalar.copy(tok_col[:], tok_ps[:, :, VS_ROW])
             tok_cols.append(tok_col)
+
+        q_codes = sb.tile([P, NQ], U32, name="q_codes", align_bytes=64)
+        q_sc = sb.tile([P, NQ], U8, name="q_sc", align_bytes=64)
+        nc.vector.quantize_mx(out=q_codes[:].bitcast(FP8X4), scales=q_sc[:], in_=q_bf[:].rearrange("p q j -> p (q j)"))
+
+        v_pool = sb.tile([P, POOL_PAGES * DV], I32, name="v_pool", tag="q_then_v", align_bytes=64)
+        nc.sync.dma_start(
+            v_pool[:].rearrange("p (u e) -> p u e", e=DV),
+            v_words.rearrange("u p e t -> p u (e t)").bitcast(I32),
+        )
 
         ks_g = sb.tile([P, N], U8, name="ks_g", tag="tok_then_ks", align_bytes=64)
         nc.vector.tensor_copy(ks_g[:], ks_pool[:].indirect(off_t[:]))
 
-        k_g = sb.tile([P, N], U32, name="k_g", tag="ks_then_keys", align_bytes=64)
+        k_g = sb.tile([P, N], U32, name="k_g", align_bytes=64)
         scores = []
         for g in range(PAGES):
             cols = slice(g * PAGE, (g + 1) * PAGE)
             nc.vector.tensor_copy(
                 k_g[:, cols], k_pool[:].bitcast(U32).indirect(off_t[:, g * PAGE // 16 : (g + 1) * PAGE // 16])
             )
-            for h in range(2):
-                part = slice(g * PAGE + h * PART, g * PAGE + (h + 1) * PART)
-                score = ps.tile([NQ, PART], F32, name=f"score{g}{h}")
-                nc.tensor.matmul_mx(
-                    out=score[:],
-                    lhsT=q_codes[:].bitcast(FP8X4),
-                    lhsT_scale=q_sc[:],
-                    rhs=k_g[:, part].bitcast(FP8X4),
-                    rhs_scale=ks_g[:, part],
-                    start=True,
-                    stop=True,
-                )
-                scores.append(score)
+            score = ps.tile([NQ, PAGE], F32, name=f"score{g}")
+            nc.tensor.matmul_mx(
+                out=score[:],
+                lhsT=q_codes[:].bitcast(FP8X4),
+                lhsT_scale=q_sc[:],
+                rhs=k_g[:, cols].bitcast(FP8X4),
+                rhs_scale=ks_g[:, cols],
+                start=True,
+                stop=True,
+            )
+            scores.append(score)
 
-        warm_src = sb.tile([P, P], F32, name="warm_src", tag="keys_then_warm", align_bytes=64)
-        nc.scalar.copy(warm_src[:], ident[:])
-        warm_ps = ps.tile([P, PACK, P], F32, name="warm_ps", tag="acc0")
-        for i in range(8):
-            nc.tensor.transpose(warm_ps[:, i % PACK, :], warm_src[:], ident[:])
+        def gather_value_scales(g, tag):
+            vsc_g = sb.tile([P, DV], U8, name=f"vsc_g{g}", tag=tag, align_bytes=64)
+            nc.vector.tensor_copy(vsc_g[:], vsc_pool[:].indirect(voff_t[:, g * DV // 16 : (g + 1) * DV // 16]))
+            return vsc_g
 
-        part_max = sb.tile([NQ, 4], F32, name="part_max", tag="max_then_vsc", align_bytes=64)
-        for i in range(4):
-            nc.vector.tensor_reduce(part_max[:, i : i + 1], scores[i][:], AX.X, ALU.max)
+        neg_first = sb.tile([NQ, 1], F32, name="neg_first")
         neg_max = sb.tile([NQ, 1], F32, name="neg_max")
-        nc.vector.tensor_reduce(neg_max[:], part_max[:], AX.X, ALU.max, negate=True)
-
-        v_g = sb.tile([P, PAGES * DV], U32, name="v_g", tag="max_then_vsc", align_bytes=64)
+        negated0 = sb.tile([NQ, PAGE], F32, name="negated0", tag="neg0_then_vsc", align_bytes=64)
+        nc.vector.tensor_scalar(negated0[:], scores[0][:], -1.0, None, ALU.mult, ALU.min, accum_out=neg_first[:])
+        vsc_gs = [gather_value_scales(0, "vsc_first")]
+        negated1 = sb.tile([NQ, PAGE], F32, name="negated1", tag="neg1_then_v", align_bytes=64)
+        nc.vector.tensor_scalar(
+            negated1[:], scores[1][:], -1.0, neg_first[:], ALU.mult, ALU.min, accum_out=neg_max[:]
+        )
+        vsc_gs.append(gather_value_scales(1, "neg0_then_vsc"))
+        v_g = sb.tile([P, PAGES * DV], U32, name="v_g", tag="neg1_then_v", align_bytes=64)
         nc.vector.tensor_copy(v_g[:], v_pool[:].bitcast(U32).indirect(voff_t[:]))
-        vsc_g = sb.tile([P, PAGES * DV], U8, name="vsc_g", tag="q_then_v", align_bytes=64)
-        nc.vector.tensor_copy(vsc_g[:], vsc_pool[:].indirect(voff_t[:]))
 
-        page_sum = sb.tile([NQ, 4], F32, name="page_sum")
-        w_bf = sb.tile([P, PAGES, NQ, PACK], BF16, name="w_bf", tag="vsc_then_v", align_bytes=64)
+        part_sum = sb.tile([NQ, 2 * PAGES], F32, name="part_sum")
+        w_bf = sb.tile([P, PAGES, NQ, PACK], BF16, name="w_bf", tag="q_then_v", align_bytes=64)
         for g in range(PAGES):
             prob = sb.tile([NQ, PACK, P], F32, name=f"prob{g}")
-            for h in range(2):
-                i = 2 * g + h
+            prob_t = ps.tile([P, PACK, NQ], F32, name=f"prob_t{g}")
+            for u in range(2):
+                pair = slice(2 * u, 2 * u + 2)
                 nc.scalar.activation(
-                    prob[:, :, h * 64 : (h + 1) * 64].rearrange("q t s -> q s t"),
-                    scores[i][:].rearrange("q (s t) -> q s t", t=PACK),
+                    prob[:, pair, :].rearrange("q t s -> q s t"),
+                    scores[g][:].rearrange("q (s t) -> q s t", t=PACK)[:, :, pair],
                     ACT.Exp,
                     bias=neg_max[:],
                     scale=1.0,
-                    accum_out=page_sum[:, i : i + 1],
+                    accum_out=part_sum[:, 2 * g + u : 2 * g + u + 1],
                 )
-            prob_t = ps.tile([P, PACK, NQ], F32, name=f"prob_t{g}", tag=f"turned{g}")
-            for t in range(PACK):
-                nc.tensor.transpose(prob_t[:, t, :], prob[:, t, :], ident[:])
+                for t in range(2 * u, 2 * u + 2):
+                    nc.tensor.transpose(prob_t[:, t, :], prob[:, t, :], ident[:])
             nc.vector.tensor_tensor(
                 w_bf[:, g],
                 prob_t[:].rearrange("s t q -> s q t"),
@@ -157,27 +165,26 @@ def tile_attend_pkv8_soft_kernel(tc, qT, k_words, k_scales, v_words, v_scales, v
             )
 
         total = sb.tile([NQ, 1], F32, name="total")
-        sum_copy = sb.tile([NQ, 4], F32, name="sum_copy")
-        nc.scalar.activation(sum_copy[:], page_sum[:], ACT.Identity, accum_out=total[:])
-        inv_total = sb.tile([NQ, 1], F32, name="inv_total", tag="tok_col0", align_bytes=64)
+        sum_copy = sb.tile([NQ, 2 * PAGES], F32, name="sum_copy")
+        nc.scalar.activation(sum_copy[:], part_sum[:], ACT.Identity, accum_out=total[:])
+        inv_total = sb.tile([NQ, 1], F32, name="inv_total")
+        nc.gpsimd.tensor_tensor(inv_total[:], total[:], minus_one[:], ALU.pow)
 
-        acc = [ps.tile([NQ, HALF], F32, name=f"acc{h}", tag=f"acc{h}") for h in range(2)]
+        acc = [ps.tile([NQ, HALF], F32, name=f"acc{h}") for h in range(2)]
         for g in range(PAGES):
             w_codes = sb.tile([P, NQ], U32, name=f"w_codes{g}", align_bytes=64)
             w_sc = sb.tile([P, NQ], U8, name=f"w_sc{g}", align_bytes=64)
             nc.vector.quantize_mx(
                 out=w_codes[:].bitcast(FP8X4), scales=w_sc[:], in_=w_bf[:, g].rearrange("s q t -> s (q t)")
             )
-            if g == 0:
-                nc.vector.reciprocal(inv_total[:], total[:])
             for h in range(2):
-                cols = slice(g * DV + h * HALF, g * DV + (h + 1) * HALF)
+                cols = slice(h * HALF, (h + 1) * HALF)
                 nc.tensor.matmul_mx(
                     out=acc[h][:],
                     lhsT=w_codes[:].bitcast(FP8X4),
                     lhsT_scale=w_sc[:],
-                    rhs=v_g[:, cols].bitcast(FP8X4),
-                    rhs_scale=vsc_g[V_ROW0:P, cols],
+                    rhs=v_g[:, g * DV + h * HALF : g * DV + (h + 1) * HALF].bitcast(FP8X4),
+                    rhs_scale=vsc_gs[g][V_ROW0:P, cols],
                     start=(g == 0),
                     stop=(g == PAGES - 1),
                 )

@@ -21,7 +21,8 @@ POOL_PAGES = T // PAGE
 V_ROW0 = 4
 VS_ROW = P - 1
 HALF = DV // 2
-ZERO_SPLIT = 2560
+KEY_ZERO_SPLIT = 384
+TOKEN_ZERO_SPLIT = 1584
 
 FLOPS = 2 * NQ * N * (D + DV)
 
@@ -36,51 +37,57 @@ def tile_attend_pkv8_soft_kernel(tc, qT, k_words, k_scales, v_words, v_scales, v
         off_t = lists.tile([P, N // 16], U16, name="off_t")
         voff_t = lists.tile([P, PAGES * DV // 16], U16, name="voff_t")
         q_raw = sb.tile([P, PACK, NQ], F32, name="q_raw", align_bytes=64)
-        ks_pool = sb.tile([P, T], U8, name="ks_pool", align_bytes=64)
+        ks_pool = sb.tile([P, T + 4], U8, name="ks_pool", align_bytes=64)
         vsc_pool = sb.tile([P, POOL_PAGES * DV], U8, name="vsc_pool", align_bytes=64)
-        tok_pool = sb.tile([P, T], F32, name="tok_pool", tag="tok_then_ks", align_bytes=64)
+        tok_pool = sb.tile([P, T + 1], F32, name="tok_pool", tag="tok_v_w", align_bytes=64)
 
-        blank = sb.tile([P, P + 1], F32, name="blank", tag="blank_then_keys", align_bytes=64)
-        nc.vector.memset(blank[:], 0.0)
-        nc.gpsimd.memset(ks_pool[:].bitcast(I32), 0)
+        blank = sb.tile([P, P], F32, name="blank", tag="blank_then_keys", align_bytes=64)
+        nc.gpsimd.memset(blank[:], 0.0)
+        nc.gpsimd.memset(ks_pool[:].bitcast(I32)[:, 0:KEY_ZERO_SPLIT], 0)
+        nc.vector.memset(ks_pool[:].bitcast(I32)[:, KEY_ZERO_SPLIT : T // 4 + 1], 0)
         ident = sb.tile([P, P], F32, name="ident")
         nc.gpsimd.affine_select(
             out=ident[:],
-            in_=blank[:, 0:P],
+            in_=blank[:],
             compare_op=ALU.not_equal,
             fill=1.0,
             base=0,
             pattern=[[-1, P]],
             channel_multiplier=1,
         )
-        nc.vector.memset(tok_pool[0:VS_ROW, 0 : ZERO_SPLIT - 1], 0.0)
-        nc.vector.memset(tok_pool[0:VS_ROW, ZERO_SPLIT - 1 : ZERO_SPLIT], 0.0)
-        nc.gpsimd.memset(tok_pool[0:VS_ROW, ZERO_SPLIT:T], 0.0)
+        nc.gpsimd.memset(tok_pool[0:VS_ROW, 0:TOKEN_ZERO_SPLIT], 0.0)
+        nc.vector.memset(tok_pool[0:VS_ROW, TOKEN_ZERO_SPLIT : T + 1], 0.0)
         nc.gpsimd.memset(vsc_pool[:].bitcast(I32), 0)
-        minus_one = sb.tile([NQ, 1], F32, name="minus_one")
-        nc.gpsimd.memset(minus_one[:], -1.0)
 
         nc.sync.dma_start(off_t[:], offs)
-        nc.scalar.dma_start(tok_pool[VS_ROW:P, :], vs[0:1, :])
         nc.scalar.dma_start(q_raw[:], qT[0].rearrange("(p j) q -> p j q", j=PACK))
+        nc.sync.dma_start(tok_pool[VS_ROW:P, 0:T], vs[0:1, :])
+        nc.sync.dma_start(voff_t[:], voffs)
         ks_rows = k_scales[0].bitcast(I32).rearrange("(a r) n -> r a n", r=4)
         for r in range(4):
-            nc.sync.dma_start(ks_pool[:].bitcast(I32)[r:P:32, :], ks_rows[r])
+            nc.sync.dma_start(ks_pool[:, 0:T].bitcast(I32)[r:P:32, :], ks_rows[r])
         k_pool = sb.tile([P, T], I32, name="k_pool", tag="blank_then_keys", align_bytes=64)
         nc.sync.dma_start(k_pool[:], k_words[0].rearrange("p n t -> p (n t)").bitcast(I32))
-        nc.sync.dma_start(voff_t[:], voffs)
+
+        q_bf = sb.tile([P, NQ, PACK], BF16, name="q_bf", align_bytes=64)
+        nc.scalar.copy(q_bf[:], q_raw[:].rearrange("p j q -> p q j"))
         vsc_rows = v_scales.bitcast(I32).rearrange("u (a r) e -> r a u e", r=4)
         for r in range(4):
-            nc.sync.dma_start(
+            nc.scalar.dma_start(
                 vsc_pool[:].bitcast(I32)[V_ROW0 + r : P : 32, :].rearrange("p (u e) -> p u e", u=POOL_PAGES),
                 vsc_rows[r],
             )
-
-        q_bf = sb.tile([P, NQ, PACK], BF16, name="q_bf", tag="q_then_v", align_bytes=64)
-        nc.scalar.copy(q_bf[:], q_raw[:].rearrange("p j q -> p q j"))
+        q_codes = sb.tile([P, NQ], U32, name="q_codes", align_bytes=64)
+        q_sc = sb.tile([P, NQ], U8, name="q_sc", align_bytes=64)
+        nc.vector.quantize_mx(out=q_codes[:].bitcast(FP8X4), scales=q_sc[:], in_=q_bf[:].rearrange("p q j -> p (q j)"))
 
         tok_g = sb.tile([P, N], F32, name="tok_g")
-        nc.vector.tensor_copy(tok_g[:], tok_pool[:].indirect(off_t[:]))
+        nc.vector.tensor_copy(tok_g[:], tok_pool[:, 0:T].indirect(off_t[:]))
+        v_pool = sb.tile([P, POOL_PAGES * DV], I32, name="v_pool", tag="tok_v_w", align_bytes=64)
+        nc.scalar.dma_start(
+            v_pool[:].rearrange("p (u e) -> p u e", e=DV),
+            v_words.rearrange("u p e t -> p u (e t)").bitcast(I32),
+        )
         tok_cols = []
         for g in range(PAGES):
             tok_ps = ps.tile([P, PACK, P], F32, name=f"tok_ps{g}")
@@ -90,33 +97,22 @@ def tile_attend_pkv8_soft_kernel(tc, qT, k_words, k_scales, v_words, v_scales, v
             nc.scalar.copy(tok_col[:], tok_ps[:, :, VS_ROW])
             tok_cols.append(tok_col)
 
-        q_codes = sb.tile([P, NQ], U32, name="q_codes", align_bytes=64)
-        q_sc = sb.tile([P, NQ], U8, name="q_sc", align_bytes=64)
-        nc.vector.quantize_mx(out=q_codes[:].bitcast(FP8X4), scales=q_sc[:], in_=q_bf[:].rearrange("p q j -> p (q j)"))
+        ks_g = sb.tile([P, N], U8, name="ks_g", align_bytes=64)
+        nc.vector.tensor_copy(ks_g[:], ks_pool[:, 0:T].indirect(off_t[:]))
 
-        v_pool = sb.tile([P, POOL_PAGES * DV], I32, name="v_pool", tag="q_then_v", align_bytes=64)
-        nc.sync.dma_start(
-            v_pool[:].rearrange("p (u e) -> p u e", e=DV),
-            v_words.rearrange("u p e t -> p u (e t)").bitcast(I32),
-        )
-
-        ks_g = sb.tile([P, N], U8, name="ks_g", tag="tok_then_ks", align_bytes=64)
-        nc.vector.tensor_copy(ks_g[:], ks_pool[:].indirect(off_t[:]))
-
-        k_g = sb.tile([P, N], U32, name="k_g", align_bytes=64)
         scores = []
         for g in range(PAGES):
-            cols = slice(g * PAGE, (g + 1) * PAGE)
+            k_g = sb.tile([P, PAGE], U32, name=f"k_g{g}", tag=f"keys{g}", align_bytes=64)
             nc.vector.tensor_copy(
-                k_g[:, cols], k_pool[:].bitcast(U32).indirect(off_t[:, g * PAGE // 16 : (g + 1) * PAGE // 16])
+                k_g[:], k_pool[:].bitcast(U32).indirect(off_t[:, g * PAGE // 16 : (g + 1) * PAGE // 16])
             )
             score = ps.tile([NQ, PAGE], F32, name=f"score{g}")
             nc.tensor.matmul_mx(
                 out=score[:],
                 lhsT=q_codes[:].bitcast(FP8X4),
                 lhsT_scale=q_sc[:],
-                rhs=k_g[:, cols].bitcast(FP8X4),
-                rhs_scale=ks_g[:, cols],
+                rhs=k_g[:].bitcast(FP8X4),
+                rhs_scale=ks_g[:, g * PAGE : (g + 1) * PAGE],
                 start=True,
                 stop=True,
             )
@@ -129,21 +125,21 @@ def tile_attend_pkv8_soft_kernel(tc, qT, k_words, k_scales, v_words, v_scales, v
 
         neg_first = sb.tile([NQ, 1], F32, name="neg_first")
         neg_max = sb.tile([NQ, 1], F32, name="neg_max")
-        negated0 = sb.tile([NQ, PAGE], F32, name="negated0", tag="neg0_then_vsc", align_bytes=64)
+        negated0 = sb.tile([NQ, PAGE], F32, name="negated0", tag="neg0_then_v", align_bytes=64)
         nc.vector.tensor_scalar(negated0[:], scores[0][:], -1.0, None, ALU.mult, ALU.min, accum_out=neg_first[:])
-        vsc_gs = [gather_value_scales(0, "vsc_first")]
-        negated1 = sb.tile([NQ, PAGE], F32, name="negated1", tag="neg1_then_v", align_bytes=64)
+        vsc_gs = [gather_value_scales(0, "keys0")]
+        negated1 = sb.tile([NQ, PAGE], F32, name="negated1", tag="neg1_then_vsc", align_bytes=64)
         nc.vector.tensor_scalar(
             negated1[:], scores[1][:], -1.0, neg_first[:], ALU.mult, ALU.min, accum_out=neg_max[:]
         )
-        vsc_gs.append(gather_value_scales(1, "neg0_then_vsc"))
-        v_g = sb.tile([P, PAGES * DV], U32, name="v_g", tag="neg1_then_v", align_bytes=64)
+        v_g = sb.tile([P, PAGES * DV], U32, name="v_g", tag="neg0_then_v", align_bytes=64)
         nc.vector.tensor_copy(v_g[:], v_pool[:].bitcast(U32).indirect(voff_t[:]))
+        vsc_gs.append(gather_value_scales(1, "neg1_then_vsc"))
 
         part_sum = sb.tile([NQ, 2 * PAGES], F32, name="part_sum")
-        w_bf = sb.tile([P, PAGES, NQ, PACK], BF16, name="w_bf", tag="q_then_v", align_bytes=64)
+        w_bf = sb.tile([P, PAGES, NQ, PACK], BF16, name="w_bf", tag="tok_v_w", align_bytes=64)
         for g in range(PAGES):
-            prob = sb.tile([NQ, PACK, P], F32, name=f"prob{g}")
+            prob = sb.tile([NQ, PACK, P], F32, name=f"prob{g}", tag=f"prob{g}", align_bytes=64)
             prob_t = ps.tile([P, PACK, NQ], F32, name=f"prob_t{g}")
             for u in range(2):
                 pair = slice(2 * u, 2 * u + 2)
@@ -167,28 +163,27 @@ def tile_attend_pkv8_soft_kernel(tc, qT, k_words, k_scales, v_words, v_scales, v
         total = sb.tile([NQ, 1], F32, name="total")
         sum_copy = sb.tile([NQ, 2 * PAGES], F32, name="sum_copy")
         nc.scalar.activation(sum_copy[:], part_sum[:], ACT.Identity, accum_out=total[:])
-        inv_total = sb.tile([NQ, 1], F32, name="inv_total")
-        nc.gpsimd.tensor_tensor(inv_total[:], total[:], minus_one[:], ALU.pow)
 
         acc = [ps.tile([NQ, HALF], F32, name=f"acc{h}") for h in range(2)]
         for g in range(PAGES):
-            w_codes = sb.tile([P, NQ], U32, name=f"w_codes{g}", align_bytes=64)
+            w_codes = sb.tile([P, NQ], U32, name=f"w_codes{g}", tag=f"prob{PAGES - 1 - g}", align_bytes=64)
             w_sc = sb.tile([P, NQ], U8, name=f"w_sc{g}", align_bytes=64)
             nc.vector.quantize_mx(
                 out=w_codes[:].bitcast(FP8X4), scales=w_sc[:], in_=w_bf[:, g].rearrange("s q t -> s (q t)")
             )
             for h in range(2):
-                cols = slice(h * HALF, (h + 1) * HALF)
                 nc.tensor.matmul_mx(
                     out=acc[h][:],
                     lhsT=w_codes[:].bitcast(FP8X4),
                     lhsT_scale=w_sc[:],
                     rhs=v_g[:, g * DV + h * HALF : g * DV + (h + 1) * HALF].bitcast(FP8X4),
-                    rhs_scale=vsc_gs[g][V_ROW0:P, cols],
+                    rhs_scale=vsc_gs[g][V_ROW0:P, h * HALF : (h + 1) * HALF],
                     start=(g == 0),
                     stop=(g == PAGES - 1),
                 )
 
+        inv_total = sb.tile([NQ, 1], F32, name="inv_total", tag="tok_v_w", align_bytes=64)
+        nc.vector.reciprocal(inv_total[:], total[:])
         y0 = sb.tile([NQ, HALF], F32, name="y0")
         nc.vector.tensor_scalar(y0[:], acc[0][:], inv_total[:], None, ALU.mult)
         nc.sync.dma_start(out[0][:, 0:HALF], y0[:])

@@ -1,6 +1,7 @@
 from contextlib import ExitStack
 
 import concourse.mybir as mybir
+from concourse.masks import make_identity
 
 F32 = mybir.dt.float32
 BF16 = mybir.dt.bfloat16
@@ -21,8 +22,8 @@ POOL_PAGES = T // PAGE
 V_ROW0 = 4
 VS_ROW = P - 1
 HALF = DV // 2
-KEY_ZERO_SPLIT = 384
-TOKEN_ZERO_SPLIT = 1584
+KEY_ZERO_SPLIT = 512
+TOKEN_ZERO_SPLIT = 1472
 
 FLOPS = 2 * NQ * N * (D + DV)
 
@@ -39,55 +40,45 @@ def tile_attend_pkv8_soft_kernel(tc, qT, k_words, k_scales, v_words, v_scales, v
         q_raw = sb.tile([P, PACK, NQ], F32, name="q_raw", align_bytes=64)
         ks_pool = sb.tile([P, T + 4], U8, name="ks_pool", align_bytes=64)
         vsc_pool = sb.tile([P, POOL_PAGES * DV], U8, name="vsc_pool", align_bytes=64)
-        tok_pool = sb.tile([P, T + 1], F32, name="tok_pool", tag="tok_v_w", align_bytes=64)
+        tok_pool = sb.tile([P, T + 1], F32, name="tok_pool", align_bytes=64)
+        k_pool = sb.tile([P, T], I32, name="k_pool", align_bytes=64)
+        v_pool = sb.tile([P, POOL_PAGES * DV], I32, name="v_pool", tag="v_then_w", align_bytes=64)
 
-        blank = sb.tile([P, P], F32, name="blank", tag="blank_then_keys", align_bytes=64)
-        nc.gpsimd.memset(blank[:], 0.0)
         nc.gpsimd.memset(ks_pool[:].bitcast(I32)[:, 0:KEY_ZERO_SPLIT], 0)
         nc.vector.memset(ks_pool[:].bitcast(I32)[:, KEY_ZERO_SPLIT : T // 4 + 1], 0)
-        ident = sb.tile([P, P], F32, name="ident")
-        nc.gpsimd.affine_select(
-            out=ident[:],
-            in_=blank[:],
-            compare_op=ALU.not_equal,
-            fill=1.0,
-            base=0,
-            pattern=[[-1, P]],
-            channel_multiplier=1,
-        )
         nc.gpsimd.memset(tok_pool[0:VS_ROW, 0:TOKEN_ZERO_SPLIT], 0.0)
         nc.vector.memset(tok_pool[0:VS_ROW, TOKEN_ZERO_SPLIT : T + 1], 0.0)
         nc.gpsimd.memset(vsc_pool[:].bitcast(I32), 0)
+        ident = sb.tile([P, P], F32, name="ident")
+        make_identity(nc, ident[:])
 
         nc.sync.dma_start(off_t[:], offs)
         nc.scalar.dma_start(q_raw[:], qT[0].rearrange("(p j) q -> p j q", j=PACK))
         nc.sync.dma_start(tok_pool[VS_ROW:P, 0:T], vs[0:1, :])
-        nc.sync.dma_start(voff_t[:], voffs)
         ks_rows = k_scales[0].bitcast(I32).rearrange("(a r) n -> r a n", r=4)
         for r in range(4):
-            nc.sync.dma_start(ks_pool[:, 0:T].bitcast(I32)[r:P:32, :], ks_rows[r])
-        k_pool = sb.tile([P, T], I32, name="k_pool", tag="blank_then_keys", align_bytes=64)
+            nc.scalar.dma_start(ks_pool[:, 0:T].bitcast(I32)[r:P:32, :], ks_rows[r])
         nc.sync.dma_start(k_pool[:], k_words[0].rearrange("p n t -> p (n t)").bitcast(I32))
-
-        q_bf = sb.tile([P, NQ, PACK], BF16, name="q_bf", align_bytes=64)
-        nc.scalar.copy(q_bf[:], q_raw[:].rearrange("p j q -> p q j"))
+        nc.sync.dma_start(voff_t[:], voffs)
         vsc_rows = v_scales.bitcast(I32).rearrange("u (a r) e -> r a u e", r=4)
         for r in range(4):
-            nc.scalar.dma_start(
+            nc.sync.dma_start(
                 vsc_pool[:].bitcast(I32)[V_ROW0 + r : P : 32, :].rearrange("p (u e) -> p u e", u=POOL_PAGES),
                 vsc_rows[r],
             )
+        nc.sync.dma_start(
+            v_pool[:].rearrange("p (u e) -> p u e", e=DV),
+            v_words.rearrange("u p e t -> p u (e t)").bitcast(I32),
+        )
+
+        q_bf = sb.tile([P, NQ, PACK], BF16, name="q_bf", align_bytes=64)
+        nc.scalar.copy(q_bf[:], q_raw[:].rearrange("p j q -> p q j"))
+        tok_g = sb.tile([P, N], F32, name="tok_g")
+        nc.vector.tensor_copy(tok_g[:], tok_pool[:, 0:T].indirect(off_t[:]))
         q_codes = sb.tile([P, NQ], U32, name="q_codes", align_bytes=64)
         q_sc = sb.tile([P, NQ], U8, name="q_sc", align_bytes=64)
         nc.vector.quantize_mx(out=q_codes[:].bitcast(FP8X4), scales=q_sc[:], in_=q_bf[:].rearrange("p q j -> p (q j)"))
 
-        tok_g = sb.tile([P, N], F32, name="tok_g")
-        nc.vector.tensor_copy(tok_g[:], tok_pool[:, 0:T].indirect(off_t[:]))
-        v_pool = sb.tile([P, POOL_PAGES * DV], I32, name="v_pool", tag="tok_v_w", align_bytes=64)
-        nc.scalar.dma_start(
-            v_pool[:].rearrange("p (u e) -> p u e", e=DV),
-            v_words.rearrange("u p e t -> p u (e t)").bitcast(I32),
-        )
         tok_cols = []
         for g in range(PAGES):
             tok_ps = ps.tile([P, PACK, P], F32, name=f"tok_ps{g}")
@@ -137,7 +128,7 @@ def tile_attend_pkv8_soft_kernel(tc, qT, k_words, k_scales, v_words, v_scales, v
         vsc_gs.append(gather_value_scales(1, "neg1_then_vsc"))
 
         part_sum = sb.tile([NQ, 2 * PAGES], F32, name="part_sum")
-        w_bf = sb.tile([P, PAGES, NQ, PACK], BF16, name="w_bf", tag="tok_v_w", align_bytes=64)
+        w_bf = sb.tile([P, PAGES, NQ, PACK], BF16, name="w_bf", tag="v_then_w", align_bytes=64)
         for g in range(PAGES):
             prob = sb.tile([NQ, PACK, P], F32, name=f"prob{g}", tag=f"prob{g}", align_bytes=64)
             prob_t = ps.tile([P, PACK, NQ], F32, name=f"prob_t{g}")
@@ -182,7 +173,7 @@ def tile_attend_pkv8_soft_kernel(tc, qT, k_words, k_scales, v_words, v_scales, v
                     stop=(g == PAGES - 1),
                 )
 
-        inv_total = sb.tile([NQ, 1], F32, name="inv_total", tag="tok_v_w", align_bytes=64)
+        inv_total = sb.tile([NQ, 1], F32, name="inv_total", tag="v_then_w", align_bytes=64)
         nc.vector.reciprocal(inv_total[:], total[:])
         y0 = sb.tile([NQ, HALF], F32, name="y0")
         nc.vector.tensor_scalar(y0[:], acc[0][:], inv_total[:], None, ALU.mult)

@@ -23,7 +23,7 @@ V_ROW0 = 4
 VS_ROW = P - 1
 HALF = DV // 2
 KEY_ZERO_SPLIT = 512
-TOKEN_ZERO_SPLIT = 1472
+TOKEN_ZERO_SPLIT = 1568
 
 FLOPS = 2 * NQ * N * (D + DV)
 
@@ -33,31 +33,34 @@ def tile_attend_pkv8_soft_kernel(tc, qT, k_words, k_scales, v_words, v_scales, v
     with ExitStack() as ctx:
         lists = ctx.enter_context(tc.tile_pool(name="lists", bufs=1))
         sb = ctx.enter_context(tc.tile_pool(name="sb", bufs=1))
+        placed = ctx.enter_context(tc.tile_pool(name="placed", bufs=1))
         ps = ctx.enter_context(tc.psum_pool(name="ps", bufs=1))
 
         off_t = lists.tile([P, N // 16], U16, name="off_t")
         voff_t = lists.tile([P, PAGES * DV // 16], U16, name="voff_t")
         q_raw = sb.tile([P, PACK, NQ], F32, name="q_raw", align_bytes=64)
-        ks_pool = sb.tile([P, T + 4], U8, name="ks_pool", align_bytes=64)
+        ks_pool = sb.tile([P, T], U8, name="ks_pool", align_bytes=64)
         vsc_pool = sb.tile([P, POOL_PAGES * DV], U8, name="vsc_pool", align_bytes=64)
-        tok_pool = sb.tile([P, T + 1], F32, name="tok_pool", align_bytes=64)
+        tok_pool = placed.tile([P, T], F32, name="tok_pool", align_bytes=64, offset=0)
         k_pool = sb.tile([P, T], I32, name="k_pool", align_bytes=64)
         v_pool = sb.tile([P, POOL_PAGES * DV], I32, name="v_pool", tag="v_then_w", align_bytes=64)
 
         nc.gpsimd.memset(ks_pool[:].bitcast(I32)[:, 0:KEY_ZERO_SPLIT], 0)
-        nc.vector.memset(ks_pool[:].bitcast(I32)[:, KEY_ZERO_SPLIT : T // 4 + 1], 0)
-        nc.gpsimd.memset(tok_pool[0:VS_ROW, 0:TOKEN_ZERO_SPLIT], 0.0)
-        nc.vector.memset(tok_pool[0:VS_ROW, TOKEN_ZERO_SPLIT : T + 1], 0.0)
-        nc.gpsimd.memset(vsc_pool[:].bitcast(I32), 0)
+        nc.vector.memset(ks_pool[:].bitcast(I32)[:, KEY_ZERO_SPLIT : T // 4 - 1], 0)
+        nc.vector.memset(ks_pool[:].bitcast(I32)[:, T // 4 - 1 : T // 4], 0)
         ident = sb.tile([P, P], F32, name="ident")
         make_identity(nc, ident[:])
+        nc.gpsimd.memset(vsc_pool[:].bitcast(I32), 0)
+        nc.gpsimd.memset(tok_pool[0:VS_ROW, 0:TOKEN_ZERO_SPLIT], 0.0)
+        nc.vector.memset(tok_pool[0:VS_ROW, TOKEN_ZERO_SPLIT : T - 1], 0.0)
+        nc.vector.memset(tok_pool[0:VS_ROW, T - 1 : T], 0.0)
 
         nc.sync.dma_start(off_t[:], offs)
-        nc.scalar.dma_start(q_raw[:], qT[0].rearrange("(p j) q -> p j q", j=PACK))
-        nc.sync.dma_start(tok_pool[VS_ROW:P, 0:T], vs[0:1, :])
+        nc.sync.dma_start(q_raw[:], qT[0].rearrange("(p j) q -> p j q", j=PACK))
+        nc.scalar.dma_start(tok_pool[VS_ROW:P, :], vs[0:1, :])
         ks_rows = k_scales[0].bitcast(I32).rearrange("(a r) n -> r a n", r=4)
         for r in range(4):
-            nc.scalar.dma_start(ks_pool[:, 0:T].bitcast(I32)[r:P:32, :], ks_rows[r])
+            nc.sync.dma_start(ks_pool[:].bitcast(I32)[r:P:32, :], ks_rows[r])
         nc.sync.dma_start(k_pool[:], k_words[0].rearrange("p n t -> p (n t)").bitcast(I32))
         nc.sync.dma_start(voff_t[:], voffs)
         vsc_rows = v_scales.bitcast(I32).rearrange("u (a r) e -> r a u e", r=4)
@@ -74,8 +77,8 @@ def tile_attend_pkv8_soft_kernel(tc, qT, k_words, k_scales, v_words, v_scales, v
         q_bf = sb.tile([P, NQ, PACK], BF16, name="q_bf", align_bytes=64)
         nc.scalar.copy(q_bf[:], q_raw[:].rearrange("p j q -> p q j"))
         tok_g = sb.tile([P, N], F32, name="tok_g")
-        nc.vector.tensor_copy(tok_g[:], tok_pool[:, 0:T].indirect(off_t[:]))
-        q_codes = sb.tile([P, NQ], U32, name="q_codes", align_bytes=64)
+        nc.vector.tensor_copy(tok_g[:], tok_pool[:].indirect(off_t[:]))
+        q_codes = placed.tile([P, NQ], U32, name="q_codes", align_bytes=64, offset=0)
         q_sc = sb.tile([P, NQ], U8, name="q_sc", align_bytes=64)
         nc.vector.quantize_mx(out=q_codes[:].bitcast(FP8X4), scales=q_sc[:], in_=q_bf[:].rearrange("p q j -> p (q j)"))
 
@@ -88,12 +91,12 @@ def tile_attend_pkv8_soft_kernel(tc, qT, k_words, k_scales, v_words, v_scales, v
             nc.scalar.copy(tok_col[:], tok_ps[:, :, VS_ROW])
             tok_cols.append(tok_col)
 
-        ks_g = sb.tile([P, N], U8, name="ks_g", align_bytes=64)
-        nc.vector.tensor_copy(ks_g[:], ks_pool[:, 0:T].indirect(off_t[:]))
+        ks_g = placed.tile([P, N], U8, name="ks_g", align_bytes=64, offset=4 * NQ)
+        nc.vector.tensor_copy(ks_g[:], ks_pool[:].indirect(off_t[:]))
 
         scores = []
         for g in range(PAGES):
-            k_g = sb.tile([P, PAGE], U32, name=f"k_g{g}", tag=f"keys{g}", align_bytes=64)
+            k_g = sb.tile([P, PAGE], U32, name=f"k_g{g}", align_bytes=64)
             nc.vector.tensor_copy(
                 k_g[:], k_pool[:].bitcast(U32).indirect(off_t[:, g * PAGE // 16 : (g + 1) * PAGE // 16])
             )
@@ -109,23 +112,18 @@ def tile_attend_pkv8_soft_kernel(tc, qT, k_words, k_scales, v_words, v_scales, v
             )
             scores.append(score)
 
-        def gather_value_scales(g, tag):
-            vsc_g = sb.tile([P, DV], U8, name=f"vsc_g{g}", tag=tag, align_bytes=64)
-            nc.vector.tensor_copy(vsc_g[:], vsc_pool[:].indirect(voff_t[:, g * DV // 16 : (g + 1) * DV // 16]))
-            return vsc_g
-
         neg_first = sb.tile([NQ, 1], F32, name="neg_first")
         neg_max = sb.tile([NQ, 1], F32, name="neg_max")
-        negated0 = sb.tile([NQ, PAGE], F32, name="negated0", tag="neg0_then_v", align_bytes=64)
+        negated0 = sb.tile([NQ, PAGE], F32, name="negated0", tag="neg0_then_vsc", align_bytes=64)
         nc.vector.tensor_scalar(negated0[:], scores[0][:], -1.0, None, ALU.mult, ALU.min, accum_out=neg_first[:])
-        vsc_gs = [gather_value_scales(0, "keys0")]
-        negated1 = sb.tile([NQ, PAGE], F32, name="negated1", tag="neg1_then_vsc", align_bytes=64)
+        negated1 = sb.tile([NQ, PAGE], F32, name="negated1", tag="neg1_then_v", align_bytes=64)
         nc.vector.tensor_scalar(
             negated1[:], scores[1][:], -1.0, neg_first[:], ALU.mult, ALU.min, accum_out=neg_max[:]
         )
-        v_g = sb.tile([P, PAGES * DV], U32, name="v_g", tag="neg0_then_v", align_bytes=64)
+        vsc_g = sb.tile([P, PAGES * DV], U8, name="vsc_g", tag="neg0_then_vsc", align_bytes=64)
+        nc.vector.tensor_copy(vsc_g[:], vsc_pool[:].indirect(voff_t[:]))
+        v_g = sb.tile([P, PAGES * DV], U32, name="v_g", tag="neg1_then_v", align_bytes=64)
         nc.vector.tensor_copy(v_g[:], v_pool[:].bitcast(U32).indirect(voff_t[:]))
-        vsc_gs.append(gather_value_scales(1, "neg1_then_vsc"))
 
         part_sum = sb.tile([NQ, 2 * PAGES], F32, name="part_sum")
         w_bf = sb.tile([P, PAGES, NQ, PACK], BF16, name="w_bf", tag="v_then_w", align_bytes=64)
@@ -168,7 +166,7 @@ def tile_attend_pkv8_soft_kernel(tc, qT, k_words, k_scales, v_words, v_scales, v
                     lhsT=w_codes[:].bitcast(FP8X4),
                     lhsT_scale=w_sc[:],
                     rhs=v_g[:, g * DV + h * HALF : g * DV + (h + 1) * HALF].bitcast(FP8X4),
-                    rhs_scale=vsc_gs[g][V_ROW0:P, h * HALF : (h + 1) * HALF],
+                    rhs_scale=vsc_g[V_ROW0:P, g * DV + h * HALF : g * DV + (h + 1) * HALF],
                     start=(g == 0),
                     stop=(g == PAGES - 1),
                 )

@@ -19,7 +19,8 @@ PAGE = 512
 N, T, D, DV, NQ = 1024, 4096, 512, 256, 128
 PAGES = N // PAGE
 POOL_PAGES = T // PAGE
-V_ROW0 = 4
+ROW_STEP = 4
+V_ROW0 = 64
 VS_ROW = P - 1
 HALF = DV // 2
 KEY_ZERO_SPLIT = 512
@@ -38,7 +39,7 @@ def tile_attend_pkv8_soft_kernel(tc, qT, k_words, k_scales, v_words, v_scales, v
 
         off_t = lists.tile([P, N // 16], U16, name="off_t")
         voff_t = lists.tile([P, PAGES * DV // 16], U16, name="voff_t")
-        q_raw = sb.tile([P, PACK, NQ], F32, name="q_raw", align_bytes=64)
+        q_raw = sb.tile([P, PACK, NQ], F32, name="q_raw", tag="q_then_plane", align_bytes=64)
         ks_pool = sb.tile([P, T], U8, name="ks_pool", align_bytes=64)
         vsc_pool = sb.tile([P, POOL_PAGES * DV], U8, name="vsc_pool", align_bytes=64)
         tok_pool = placed.tile([P, T], F32, name="tok_pool", align_bytes=64, offset=0)
@@ -58,17 +59,13 @@ def tile_attend_pkv8_soft_kernel(tc, qT, k_words, k_scales, v_words, v_scales, v
         nc.sync.dma_start(off_t[:], offs)
         nc.sync.dma_start(q_raw[:], qT[0].rearrange("(p j) q -> p j q", j=PACK))
         nc.scalar.dma_start(tok_pool[VS_ROW:P, :], vs[0:1, :])
-        ks_rows = k_scales[0].bitcast(I32).rearrange("(a r) n -> r a n", r=4)
-        for r in range(4):
-            nc.sync.dma_start(ks_pool[:].bitcast(I32)[r:P:32, :], ks_rows[r])
+        nc.sync.dma_start(ks_pool[:].bitcast(I32)[0:V_ROW0:ROW_STEP, :], k_scales[0].bitcast(I32))
         nc.sync.dma_start(k_pool[:], k_words[0].rearrange("p n t -> p (n t)").bitcast(I32))
         nc.sync.dma_start(voff_t[:], voffs)
-        vsc_rows = v_scales.bitcast(I32).rearrange("u (a r) e -> r a u e", r=4)
-        for r in range(4):
-            nc.sync.dma_start(
-                vsc_pool[:].bitcast(I32)[V_ROW0 + r : P : 32, :].rearrange("p (u e) -> p u e", u=POOL_PAGES),
-                vsc_rows[r],
-            )
+        nc.sync.dma_start(
+            vsc_pool[:].bitcast(I32)[V_ROW0:P:ROW_STEP, :].rearrange("p (u e) -> p u e", u=POOL_PAGES),
+            v_scales.bitcast(I32).rearrange("u f e -> f u e"),
+        )
         nc.sync.dma_start(
             v_pool[:].rearrange("p (u e) -> p u e", e=DV),
             v_words.rearrange("u p e t -> p u (e t)").bitcast(I32),
@@ -76,8 +73,21 @@ def tile_attend_pkv8_soft_kernel(tc, qT, k_words, k_scales, v_words, v_scales, v
 
         q_bf = sb.tile([P, NQ, PACK], BF16, name="q_bf", align_bytes=64)
         nc.scalar.copy(q_bf[:], q_raw[:].rearrange("p j q -> p q j"))
-        tok_g = sb.tile([P, N], F32, name="tok_g")
-        nc.vector.tensor_copy(tok_g[:], tok_pool[:].indirect(off_t[:]))
+        ks_g = sb.tile([P, N], U8, name="ks_g", align_bytes=64)
+        nc.vector.tensor_copy(ks_g[:], ks_pool[:].indirect(off_t[:]))
+        ks_plane = sb.tile([P, N], U8, name="ks_plane", tag="q_then_plane", align_bytes=64)
+        for r in range(4):
+            nc.scalar.dma_start(
+                ks_plane[:].bitcast(I32)[r:P:32, :],
+                ks_g[:].bitcast(I32)[ROW_STEP * r : V_ROW0 : 4 * ROW_STEP, :],
+            )
+        tok_gs = []
+        for g in range(PAGES):
+            tok_g = sb.tile([P, PAGE], F32, name=f"tok_g{g}")
+            nc.vector.tensor_copy(
+                tok_g[:], tok_pool[:].indirect(off_t[:, g * PAGE // 16 : (g + 1) * PAGE // 16])
+            )
+            tok_gs.append(tok_g)
         q_codes = placed.tile([P, NQ], U32, name="q_codes", align_bytes=64, offset=0)
         q_sc = sb.tile([P, NQ], U8, name="q_sc", align_bytes=64)
         nc.vector.quantize_mx(out=q_codes[:].bitcast(FP8X4), scales=q_sc[:], in_=q_bf[:].rearrange("p q j -> p (q j)"))
@@ -86,17 +96,14 @@ def tile_attend_pkv8_soft_kernel(tc, qT, k_words, k_scales, v_words, v_scales, v
         for g in range(PAGES):
             tok_ps = ps.tile([P, PACK, P], F32, name=f"tok_ps{g}")
             for t in range(PACK):
-                nc.tensor.transpose(tok_ps[:, t, :], tok_g[:, g * PAGE + t : (g + 1) * PAGE : PACK], ident[:])
+                nc.tensor.transpose(tok_ps[:, t, :], tok_gs[g][:, t:PAGE:PACK], ident[:])
             tok_col = sb.tile([P, PACK], F32, name=f"tok_col{g}", align_bytes=64)
             nc.scalar.copy(tok_col[:], tok_ps[:, :, VS_ROW])
             tok_cols.append(tok_col)
 
-        ks_g = placed.tile([P, N], U8, name="ks_g", align_bytes=64, offset=4 * NQ)
-        nc.vector.tensor_copy(ks_g[:], ks_pool[:].indirect(off_t[:]))
-
         scores = []
         for g in range(PAGES):
-            k_g = sb.tile([P, PAGE], U32, name=f"k_g{g}", align_bytes=64)
+            k_g = placed.tile([P, PAGE], U32, name=f"k_g{g}", align_bytes=64, offset=4 * PAGE * (g + 1))
             nc.vector.tensor_copy(
                 k_g[:], k_pool[:].bitcast(U32).indirect(off_t[:, g * PAGE // 16 : (g + 1) * PAGE // 16])
             )
@@ -106,7 +113,7 @@ def tile_attend_pkv8_soft_kernel(tc, qT, k_words, k_scales, v_words, v_scales, v
                 lhsT=q_codes[:].bitcast(FP8X4),
                 lhsT_scale=q_sc[:],
                 rhs=k_g[:].bitcast(FP8X4),
-                rhs_scale=ks_g[:, g * PAGE : (g + 1) * PAGE],
+                rhs_scale=ks_plane[:, g * PAGE : (g + 1) * PAGE],
                 start=True,
                 stop=True,
             )
@@ -122,6 +129,12 @@ def tile_attend_pkv8_soft_kernel(tc, qT, k_words, k_scales, v_words, v_scales, v
         )
         vsc_g = sb.tile([P, PAGES * DV], U8, name="vsc_g", tag="neg0_then_vsc", align_bytes=64)
         nc.vector.tensor_copy(vsc_g[:], vsc_pool[:].indirect(voff_t[:]))
+        vsc_plane = sb.tile([P, PAGES * DV], U8, name="vsc_plane", align_bytes=64)
+        for r in range(4):
+            nc.sync.dma_start(
+                vsc_plane[:].bitcast(I32)[r:P:32, :],
+                vsc_g[:].bitcast(I32)[V_ROW0 + ROW_STEP * r : P : 4 * ROW_STEP, :],
+            )
         v_g = sb.tile([P, PAGES * DV], U32, name="v_g", tag="neg1_then_v", align_bytes=64)
         nc.vector.tensor_copy(v_g[:], v_pool[:].bitcast(U32).indirect(voff_t[:]))
 
@@ -166,7 +179,7 @@ def tile_attend_pkv8_soft_kernel(tc, qT, k_words, k_scales, v_words, v_scales, v
                     lhsT=w_codes[:].bitcast(FP8X4),
                     lhsT_scale=w_sc[:],
                     rhs=v_g[:, g * DV + h * HALF : g * DV + (h + 1) * HALF].bitcast(FP8X4),
-                    rhs_scale=vsc_g[V_ROW0:P, g * DV + h * HALF : g * DV + (h + 1) * HALF],
+                    rhs_scale=vsc_plane[:, g * DV + h * HALF : g * DV + (h + 1) * HALF],
                     start=(g == 0),
                     stop=(g == PAGES - 1),
                 )

@@ -39,12 +39,11 @@ def tile_attend_pkv8_soft_kernel(tc, qT, k_words, k_scales, v_words, v_scales, v
 
         off_t = lists.tile([P, N // 16], U16, name="off_t")
         voff_t = lists.tile([P, PAGES * DV // 16], U16, name="voff_t")
-        q_raw = sb.tile([P, PACK, NQ], F32, name="q_raw", tag="q_then_plane", align_bytes=64)
-        ks_pool = sb.tile([P, T], U8, name="ks_pool", align_bytes=64)
+        q_raw = sb.tile([P, PACK, NQ], F32, name="q_raw", align_bytes=64)
+        ks_pool = sb.tile([P, T], U8, name="ks_pool", tag="v_then_w", align_bytes=64)
         vsc_pool = sb.tile([P, POOL_PAGES * DV], U8, name="vsc_pool", align_bytes=64)
         tok_pool = placed.tile([P, T], F32, name="tok_pool", align_bytes=64, offset=0)
         k_pool = sb.tile([P, T], I32, name="k_pool", align_bytes=64)
-        v_pool = sb.tile([P, POOL_PAGES * DV], I32, name="v_pool", tag="v_then_w", align_bytes=64)
 
         nc.gpsimd.memset(ks_pool[:].bitcast(I32)[:, 0:KEY_ZERO_SPLIT], 0)
         nc.vector.memset(ks_pool[:].bitcast(I32)[:, KEY_ZERO_SPLIT : T // 4 - 1], 0)
@@ -66,21 +65,22 @@ def tile_attend_pkv8_soft_kernel(tc, qT, k_words, k_scales, v_words, v_scales, v
             vsc_pool[:].bitcast(I32)[V_ROW0:P:ROW_STEP, :].rearrange("p (u e) -> p u e", u=POOL_PAGES),
             v_scales.bitcast(I32).rearrange("u f e -> f u e"),
         )
-        nc.sync.dma_start(
-            v_pool[:].rearrange("p (u e) -> p u e", e=DV),
-            v_words.rearrange("u p e t -> p u (e t)").bitcast(I32),
-        )
 
         q_bf = sb.tile([P, NQ, PACK], BF16, name="q_bf", align_bytes=64)
         nc.scalar.copy(q_bf[:], q_raw[:].rearrange("p j q -> p q j"))
         ks_g = sb.tile([P, N], U8, name="ks_g", align_bytes=64)
         nc.vector.tensor_copy(ks_g[:], ks_pool[:].indirect(off_t[:]))
-        ks_plane = sb.tile([P, N], U8, name="ks_plane", tag="q_then_plane", align_bytes=64)
+        ks_plane = sb.tile([P, N], U8, name="ks_plane", align_bytes=64)
         for r in range(4):
-            nc.scalar.dma_start(
+            nc.sync.dma_start(
                 ks_plane[:].bitcast(I32)[r:P:32, :],
                 ks_g[:].bitcast(I32)[ROW_STEP * r : V_ROW0 : 4 * ROW_STEP, :],
             )
+        v_pool = sb.tile([P, POOL_PAGES * DV], I32, name="v_pool", tag="v_then_w", align_bytes=64)
+        nc.sync.dma_start(
+            v_pool[:].rearrange("p (u e) -> p u e", e=DV),
+            v_words.rearrange("u p e t -> p u (e t)").bitcast(I32),
+        )
         tok_gs = []
         for g in range(PAGES):
             tok_g = sb.tile([P, PAGE], F32, name=f"tok_g{g}")

@@ -20,11 +20,15 @@ N, T, D, DV, NQ = 1024, 4096, 512, 256, 128
 PAGES = N // PAGE
 POOL_PAGES = T // PAGE
 ROW_STEP = 4
-V_ROW0 = 64
+K_ROW0 = 32
+K_ROW_END = 96
+SPARE = 8
+SEED = 16
+FILL_END = 1504
 VS_ROW = P - 1
 HALF = DV // 2
 KEY_ZERO_SPLIT = 512
-TOKEN_ZERO_SPLIT = 1568
+TOKEN_ZERO_SPLIT = 2200
 
 FLOPS = 2 * NQ * N * (D + DV)
 
@@ -34,61 +38,67 @@ def tile_attend_pkv8_soft_kernel(tc, qT, k_words, k_scales, v_words, v_scales, v
     with ExitStack() as ctx:
         lists = ctx.enter_context(tc.tile_pool(name="lists", bufs=1))
         sb = ctx.enter_context(tc.tile_pool(name="sb", bufs=1))
-        placed = ctx.enter_context(tc.tile_pool(name="placed", bufs=1))
         ps = ctx.enter_context(tc.psum_pool(name="ps", bufs=1))
 
         off_t = lists.tile([P, N // 16], U16, name="off_t")
         voff_t = lists.tile([P, PAGES * DV // 16], U16, name="voff_t")
         q_raw = sb.tile([P, PACK, NQ], F32, name="q_raw", align_bytes=64)
-        ks_pool = sb.tile([P, T], U8, name="ks_pool", tag="v_then_w", align_bytes=64)
-        vsc_pool = sb.tile([P, POOL_PAGES * DV], U8, name="vsc_pool", align_bytes=64)
-        tok_pool = placed.tile([P, T], F32, name="tok_pool", align_bytes=64, offset=0)
+        ks_pool = sb.tile([P, T + 4 * SPARE], U8, name="ks_pool", tag="ks_then_v", align_bytes=64)
+        tok_pool = sb.tile([P, T + SPARE], F32, name="tok_pool", align_bytes=64)
         k_pool = sb.tile([P, T], I32, name="k_pool", align_bytes=64)
+        vsc_pool = sb.tile([P, POOL_PAGES * DV], U8, name="vsc_pool", tag="vsc_then_w", align_bytes=64)
 
         nc.gpsimd.memset(ks_pool[:].bitcast(I32)[:, 0:KEY_ZERO_SPLIT], 0)
-        nc.vector.memset(ks_pool[:].bitcast(I32)[:, KEY_ZERO_SPLIT : T // 4 - 1], 0)
-        nc.vector.memset(ks_pool[:].bitcast(I32)[:, T // 4 - 1 : T // 4], 0)
+        nc.vector.memset(ks_pool[:].bitcast(I32)[:, KEY_ZERO_SPLIT : T // 4 + 1], 0)
         ident = sb.tile([P, P], F32, name="ident")
         make_identity(nc, ident[:])
         nc.gpsimd.memset(vsc_pool[:].bitcast(I32), 0)
-        nc.gpsimd.memset(tok_pool[0:VS_ROW, 0:TOKEN_ZERO_SPLIT], 0.0)
-        nc.vector.memset(tok_pool[0:VS_ROW, TOKEN_ZERO_SPLIT : T - 1], 0.0)
-        nc.vector.memset(tok_pool[0:VS_ROW, T - 1 : T], 0.0)
+        nc.gpsimd.memset(tok_pool[0:VS_ROW, FILL_END:TOKEN_ZERO_SPLIT], 0.0)
+        nc.vector.memset(tok_pool[0:VS_ROW, TOKEN_ZERO_SPLIT : T + 1], 0.0)
 
-        nc.sync.dma_start(off_t[:], offs)
         nc.sync.dma_start(q_raw[:], qT[0].rearrange("(p j) q -> p j q", j=PACK))
-        nc.scalar.dma_start(tok_pool[VS_ROW:P, :], vs[0:1, :])
-        nc.sync.dma_start(ks_pool[:].bitcast(I32)[0:V_ROW0:ROW_STEP, :], k_scales[0].bitcast(I32))
+        nc.sync.dma_start(off_t[:], offs)
+        seed = sb.tile([P, SEED], F32, name="seed", align_bytes=64)
+        nc.scalar.dma_start(seed[:], vs[:, 0:SEED])
+        nc.sync.dma_start(ks_pool[:].bitcast(I32)[K_ROW0:K_ROW_END:ROW_STEP, 0 : T // 4], k_scales[0].bitcast(I32))
+        nc.sync.dma_start(tok_pool[VS_ROW:P, 0:T], vs[0:1, :])
         nc.sync.dma_start(k_pool[:], k_words[0].rearrange("p n t -> p (n t)").bitcast(I32))
         nc.sync.dma_start(voff_t[:], voffs)
-        nc.sync.dma_start(
-            vsc_pool[:].bitcast(I32)[V_ROW0:P:ROW_STEP, :].rearrange("p (u e) -> p u e", u=POOL_PAGES),
-            v_scales.bitcast(I32).rearrange("u f e -> f u e"),
-        )
 
         q_bf = sb.tile([P, NQ, PACK], BF16, name="q_bf", align_bytes=64)
         nc.scalar.copy(q_bf[:], q_raw[:].rearrange("p j q -> p q j"))
+        nc.scalar.activation(
+            tok_pool[0:VS_ROW, 0:FILL_END].rearrange("p (n c) -> p n c", c=SEED),
+            seed[0:VS_ROW, :].unsqueeze(1).to_broadcast([VS_ROW, FILL_END // SEED, SEED]),
+            ACT.Copy,
+        )
         ks_g = sb.tile([P, N], U8, name="ks_g", align_bytes=64)
-        nc.vector.tensor_copy(ks_g[:], ks_pool[:].indirect(off_t[:]))
+        nc.vector.tensor_copy(ks_g[:], ks_pool[:, 0:T].indirect(off_t[:]))
         ks_plane = sb.tile([P, N], U8, name="ks_plane", align_bytes=64)
         for r in range(4):
             nc.sync.dma_start(
                 ks_plane[:].bitcast(I32)[r:P:32, :],
-                ks_g[:].bitcast(I32)[ROW_STEP * r : V_ROW0 : 4 * ROW_STEP, :],
+                ks_g[:].bitcast(I32)[K_ROW0 + ROW_STEP * r : K_ROW_END : 4 * ROW_STEP, :],
             )
-        v_pool = sb.tile([P, POOL_PAGES * DV], I32, name="v_pool", tag="v_then_w", align_bytes=64)
+        v_pool = sb.tile([P, POOL_PAGES * DV], I32, name="v_pool", tag="ks_then_v", align_bytes=64)
         nc.sync.dma_start(
             v_pool[:].rearrange("p (u e) -> p u e", e=DV),
             v_words.rearrange("u p e t -> p u (e t)").bitcast(I32),
         )
+        vsc_rows = v_scales.bitcast(I32).rearrange("u (a r) e -> r a u e", r=4)
+        for r in range(4):
+            nc.sync.dma_start(
+                vsc_pool[:].bitcast(I32)[r:P:32, :].rearrange("p (u e) -> p u e", u=POOL_PAGES),
+                vsc_rows[r],
+            )
         tok_gs = []
         for g in range(PAGES):
             tok_g = sb.tile([P, PAGE], F32, name=f"tok_g{g}")
             nc.vector.tensor_copy(
-                tok_g[:], tok_pool[:].indirect(off_t[:, g * PAGE // 16 : (g + 1) * PAGE // 16])
+                tok_g[:], tok_pool[:, 0:T].indirect(off_t[:, g * PAGE // 16 : (g + 1) * PAGE // 16])
             )
             tok_gs.append(tok_g)
-        q_codes = placed.tile([P, NQ], U32, name="q_codes", align_bytes=64, offset=0)
+        q_codes = sb.tile([P, NQ], U32, name="q_codes", align_bytes=64)
         q_sc = sb.tile([P, NQ], U8, name="q_sc", align_bytes=64)
         nc.vector.quantize_mx(out=q_codes[:].bitcast(FP8X4), scales=q_sc[:], in_=q_bf[:].rearrange("p q j -> p (q j)"))
 
@@ -103,7 +113,7 @@ def tile_attend_pkv8_soft_kernel(tc, qT, k_words, k_scales, v_words, v_scales, v
 
         scores = []
         for g in range(PAGES):
-            k_g = placed.tile([P, PAGE], U32, name=f"k_g{g}", align_bytes=64, offset=4 * PAGE * (g + 1))
+            k_g = sb.tile([P, PAGE], U32, name=f"k_g{g}", align_bytes=64)
             nc.vector.tensor_copy(
                 k_g[:], k_pool[:].bitcast(U32).indirect(off_t[:, g * PAGE // 16 : (g + 1) * PAGE // 16])
             )
@@ -127,19 +137,13 @@ def tile_attend_pkv8_soft_kernel(tc, qT, k_words, k_scales, v_words, v_scales, v
         nc.vector.tensor_scalar(
             negated1[:], scores[1][:], -1.0, neg_first[:], ALU.mult, ALU.min, accum_out=neg_max[:]
         )
-        vsc_g = sb.tile([P, PAGES * DV], U8, name="vsc_g", tag="neg0_then_vsc", align_bytes=64)
-        nc.vector.tensor_copy(vsc_g[:], vsc_pool[:].indirect(voff_t[:]))
-        vsc_plane = sb.tile([P, PAGES * DV], U8, name="vsc_plane", align_bytes=64)
-        for r in range(4):
-            nc.sync.dma_start(
-                vsc_plane[:].bitcast(I32)[r:P:32, :],
-                vsc_g[:].bitcast(I32)[V_ROW0 + ROW_STEP * r : P : 4 * ROW_STEP, :],
-            )
-        v_g = sb.tile([P, PAGES * DV], U32, name="v_g", tag="neg1_then_v", align_bytes=64)
+        v_g = sb.tile([P, PAGES * DV], U32, name="v_g", tag="neg0_then_vsc", align_bytes=64)
         nc.vector.tensor_copy(v_g[:], v_pool[:].bitcast(U32).indirect(voff_t[:]))
+        vsc_g = sb.tile([P, PAGES * DV], U8, name="vsc_g", tag="neg1_then_v", align_bytes=64)
+        nc.vector.tensor_copy(vsc_g[:], vsc_pool[:].indirect(voff_t[:]))
 
         part_sum = sb.tile([NQ, 2 * PAGES], F32, name="part_sum")
-        w_bf = sb.tile([P, PAGES, NQ, PACK], BF16, name="w_bf", tag="v_then_w", align_bytes=64)
+        w_bf = sb.tile([P, PAGES, NQ, PACK], BF16, name="w_bf", tag="vsc_then_w", align_bytes=64)
         for g in range(PAGES):
             prob = sb.tile([NQ, PACK, P], F32, name=f"prob{g}", tag=f"prob{g}", align_bytes=64)
             prob_t = ps.tile([P, PACK, NQ], F32, name=f"prob_t{g}")
@@ -179,12 +183,12 @@ def tile_attend_pkv8_soft_kernel(tc, qT, k_words, k_scales, v_words, v_scales, v
                     lhsT=w_codes[:].bitcast(FP8X4),
                     lhsT_scale=w_sc[:],
                     rhs=v_g[:, g * DV + h * HALF : g * DV + (h + 1) * HALF].bitcast(FP8X4),
-                    rhs_scale=vsc_plane[:, g * DV + h * HALF : g * DV + (h + 1) * HALF],
+                    rhs_scale=vsc_g[:, g * DV + h * HALF : g * DV + (h + 1) * HALF],
                     start=(g == 0),
                     stop=(g == PAGES - 1),
                 )
 
-        inv_total = sb.tile([NQ, 1], F32, name="inv_total", tag="v_then_w", align_bytes=64)
+        inv_total = sb.tile([NQ, 1], F32, name="inv_total", tag="vsc_then_w", align_bytes=64)
         nc.vector.reciprocal(inv_total[:], total[:])
         y0 = sb.tile([NQ, HALF], F32, name="y0")
         nc.vector.tensor_scalar(y0[:], acc[0][:], inv_total[:], None, ALU.mult)

@@ -22,13 +22,10 @@ POOL_PAGES = T // PAGE
 ROW_STEP = 4
 K_ROW0 = 32
 K_ROW_END = 96
-SPARE = 8
-SEED = 16
-FILL_END = 1504
 VS_ROW = P - 1
 HALF = DV // 2
 KEY_ZERO_SPLIT = 512
-TOKEN_ZERO_SPLIT = 2200
+TOKEN_ZERO_SPLIT = 1568
 
 FLOPS = 2 * NQ * N * (D + DV)
 
@@ -43,37 +40,32 @@ def tile_attend_pkv8_soft_kernel(tc, qT, k_words, k_scales, v_words, v_scales, v
         off_t = lists.tile([P, N // 16], U16, name="off_t")
         voff_t = lists.tile([P, PAGES * DV // 16], U16, name="voff_t")
         q_raw = sb.tile([P, PACK, NQ], F32, name="q_raw", align_bytes=64)
-        ks_pool = sb.tile([P, T + 4 * SPARE], U8, name="ks_pool", tag="ks_then_v", align_bytes=64)
-        tok_pool = sb.tile([P, T + SPARE], F32, name="tok_pool", align_bytes=64)
+        ks_pool = sb.tile([P, T], U8, name="ks_pool", tag="ks_then_v", align_bytes=64)
+        tok_pool = sb.tile([P, T], F32, name="tok_pool", align_bytes=64)
         k_pool = sb.tile([P, T], I32, name="k_pool", align_bytes=64)
         vsc_pool = sb.tile([P, POOL_PAGES * DV], U8, name="vsc_pool", tag="vsc_then_w", align_bytes=64)
 
         nc.gpsimd.memset(ks_pool[:].bitcast(I32)[:, 0:KEY_ZERO_SPLIT], 0)
-        nc.vector.memset(ks_pool[:].bitcast(I32)[:, KEY_ZERO_SPLIT : T // 4 + 1], 0)
+        nc.vector.memset(ks_pool[:].bitcast(I32)[:, KEY_ZERO_SPLIT : T // 4 - 1], 0)
+        nc.vector.memset(ks_pool[:].bitcast(I32)[:, T // 4 - 1 : T // 4], 0)
         ident = sb.tile([P, P], F32, name="ident")
         make_identity(nc, ident[:])
         nc.gpsimd.memset(vsc_pool[:].bitcast(I32), 0)
-        nc.gpsimd.memset(tok_pool[0:VS_ROW, FILL_END:TOKEN_ZERO_SPLIT], 0.0)
-        nc.vector.memset(tok_pool[0:VS_ROW, TOKEN_ZERO_SPLIT : T + 1], 0.0)
+        nc.gpsimd.memset(tok_pool[0:VS_ROW, 0:TOKEN_ZERO_SPLIT], 0.0)
+        nc.vector.memset(tok_pool[0:VS_ROW, TOKEN_ZERO_SPLIT : T - 1], 0.0)
+        nc.vector.memset(tok_pool[0:VS_ROW, T - 1 : T], 0.0)
 
         nc.sync.dma_start(q_raw[:], qT[0].rearrange("(p j) q -> p j q", j=PACK))
         nc.sync.dma_start(off_t[:], offs)
-        seed = sb.tile([P, SEED], F32, name="seed", align_bytes=64)
-        nc.scalar.dma_start(seed[:], vs[:, 0:SEED])
-        nc.sync.dma_start(ks_pool[:].bitcast(I32)[K_ROW0:K_ROW_END:ROW_STEP, 0 : T // 4], k_scales[0].bitcast(I32))
-        nc.sync.dma_start(tok_pool[VS_ROW:P, 0:T], vs[0:1, :])
+        nc.sync.dma_start(ks_pool[:].bitcast(I32)[K_ROW0:K_ROW_END:ROW_STEP, :], k_scales[0].bitcast(I32))
+        nc.sync.dma_start(tok_pool[VS_ROW:P, :], vs[0:1, :])
         nc.sync.dma_start(k_pool[:], k_words[0].rearrange("p n t -> p (n t)").bitcast(I32))
         nc.sync.dma_start(voff_t[:], voffs)
 
         q_bf = sb.tile([P, NQ, PACK], BF16, name="q_bf", align_bytes=64)
         nc.scalar.copy(q_bf[:], q_raw[:].rearrange("p j q -> p q j"))
-        nc.scalar.activation(
-            tok_pool[0:VS_ROW, 0:FILL_END].rearrange("p (n c) -> p n c", c=SEED),
-            seed[0:VS_ROW, :].unsqueeze(1).to_broadcast([VS_ROW, FILL_END // SEED, SEED]),
-            ACT.Copy,
-        )
         ks_g = sb.tile([P, N], U8, name="ks_g", align_bytes=64)
-        nc.vector.tensor_copy(ks_g[:], ks_pool[:, 0:T].indirect(off_t[:]))
+        nc.vector.tensor_copy(ks_g[:], ks_pool[:].indirect(off_t[:]))
         ks_plane = sb.tile([P, N], U8, name="ks_plane", align_bytes=64)
         for r in range(4):
             nc.sync.dma_start(
@@ -95,7 +87,7 @@ def tile_attend_pkv8_soft_kernel(tc, qT, k_words, k_scales, v_words, v_scales, v
         for g in range(PAGES):
             tok_g = sb.tile([P, PAGE], F32, name=f"tok_g{g}")
             nc.vector.tensor_copy(
-                tok_g[:], tok_pool[:, 0:T].indirect(off_t[:, g * PAGE // 16 : (g + 1) * PAGE // 16])
+                tok_g[:], tok_pool[:].indirect(off_t[:, g * PAGE // 16 : (g + 1) * PAGE // 16])
             )
             tok_gs.append(tok_g)
         q_codes = sb.tile([P, NQ], U32, name="q_codes", align_bytes=64)

@@ -86,8 +86,8 @@ def tile_attend_pkv8_soft_kernel(tc, qT, k_words, k_scales, v_words, v_scales, v
         tok_gs = []
         for g in range(PAGES):
             tok_g = sb.tile([P, PAGE], F32, name=f"tok_g{g}")
-            nc.vector.tensor_copy(
-                tok_g[:], tok_pool[:].indirect(off_t[:, g * PAGE // 16 : (g + 1) * PAGE // 16])
+            nc.scalar.activation(
+                tok_g[:], tok_pool[:].indirect(off_t[:, g * PAGE // 16 : (g + 1) * PAGE // 16]), ACT.Copy
             )
             tok_gs.append(tok_g)
         q_codes = sb.tile([P, NQ], U32, name="q_codes", align_bytes=64)

@@ -24,8 +24,9 @@ K_ROW0 = 32
 K_ROW_END = 96
 VS_ROW = P - 1
 HALF = DV // 2
+VSC_AT = NQ + 4 * P
 KEY_ZERO_SPLIT = 512
-TOKEN_ZERO_SPLIT = 1568
+TOKEN_ZERO_SPLIT = 2000
 
 FLOPS = 2 * NQ * N * (D + DV)
 
@@ -35,22 +36,19 @@ def tile_attend_pkv8_soft_kernel(tc, qT, k_words, k_scales, v_words, v_scales, v
     with ExitStack() as ctx:
         lists = ctx.enter_context(tc.tile_pool(name="lists", bufs=1))
         sb = ctx.enter_context(tc.tile_pool(name="sb", bufs=1))
+        shared = ctx.enter_context(tc.tile_pool(name="shared", bufs=1))
         ps = ctx.enter_context(tc.psum_pool(name="ps", bufs=1))
 
         off_t = lists.tile([P, N // 16], U16, name="off_t")
         voff_t = lists.tile([P, PAGES * DV // 16], U16, name="voff_t")
         q_raw = sb.tile([P, PACK, NQ], F32, name="q_raw", align_bytes=64)
-        ks_pool = sb.tile([P, T], U8, name="ks_pool", tag="ks_then_v", align_bytes=64)
+        ks_pool = shared.tile([P, T], U8, name="ks_pool", offset=0, align_bytes=64)
         tok_pool = sb.tile([P, T], F32, name="tok_pool", align_bytes=64)
         k_pool = sb.tile([P, T], I32, name="k_pool", align_bytes=64)
-        vsc_pool = sb.tile([P, POOL_PAGES * DV], U8, name="vsc_pool", tag="vsc_then_w", align_bytes=64)
 
         nc.gpsimd.memset(ks_pool[:].bitcast(I32)[:, 0:KEY_ZERO_SPLIT], 0)
         nc.vector.memset(ks_pool[:].bitcast(I32)[:, KEY_ZERO_SPLIT : T // 4 - 1], 0)
         nc.vector.memset(ks_pool[:].bitcast(I32)[:, T // 4 - 1 : T // 4], 0)
-        ident = sb.tile([P, P], F32, name="ident")
-        make_identity(nc, ident[:])
-        nc.gpsimd.memset(vsc_pool[:].bitcast(I32), 0)
         nc.gpsimd.memset(tok_pool[0:VS_ROW, 0:TOKEN_ZERO_SPLIT], 0.0)
         nc.vector.memset(tok_pool[0:VS_ROW, TOKEN_ZERO_SPLIT : T - 1], 0.0)
         nc.vector.memset(tok_pool[0:VS_ROW, T - 1 : T], 0.0)
@@ -66,13 +64,17 @@ def tile_attend_pkv8_soft_kernel(tc, qT, k_words, k_scales, v_words, v_scales, v
         nc.scalar.copy(q_bf[:], q_raw[:].rearrange("p j q -> p q j"))
         ks_g = sb.tile([P, N], U8, name="ks_g", align_bytes=64)
         nc.vector.tensor_copy(ks_g[:], ks_pool[:].indirect(off_t[:]))
+        ident = shared.tile([P, P], F32, name="ident", offset=NQ, align_bytes=64)
+        make_identity(nc, ident[:])
+        vsc_pool = shared.tile([P, POOL_PAGES * DV], U8, name="vsc_pool", offset=VSC_AT, align_bytes=64)
+        nc.vector.memset(vsc_pool[:].bitcast(I32), 0)
         ks_plane = sb.tile([P, N], U8, name="ks_plane", align_bytes=64)
         for r in range(4):
             nc.sync.dma_start(
                 ks_plane[:].bitcast(I32)[r:P:32, :],
                 ks_g[:].bitcast(I32)[K_ROW0 + ROW_STEP * r : K_ROW_END : 4 * ROW_STEP, :],
             )
-        v_pool = sb.tile([P, POOL_PAGES * DV], I32, name="v_pool", tag="ks_then_v", align_bytes=64)
+        v_pool = sb.tile([P, POOL_PAGES * DV], I32, name="v_pool", align_bytes=64)
         nc.sync.dma_start(
             v_pool[:].rearrange("p (u e) -> p u e", e=DV),
             v_words.rearrange("u p e t -> p u (e t)").bitcast(I32),
@@ -91,7 +93,7 @@ def tile_attend_pkv8_soft_kernel(tc, qT, k_words, k_scales, v_words, v_scales, v
             )
             tok_gs.append(tok_g)
         q_codes = sb.tile([P, NQ], U32, name="q_codes", align_bytes=64)
-        q_sc = sb.tile([P, NQ], U8, name="q_sc", align_bytes=64)
+        q_sc = shared.tile([P, NQ], U8, name="q_sc", offset=0, align_bytes=64)
         nc.vector.quantize_mx(out=q_codes[:].bitcast(FP8X4), scales=q_sc[:], in_=q_bf[:].rearrange("p q j -> p (q j)"))
 
         tok_cols = []
@@ -135,7 +137,7 @@ def tile_attend_pkv8_soft_kernel(tc, qT, k_words, k_scales, v_words, v_scales, v
         nc.vector.tensor_copy(vsc_g[:], vsc_pool[:].indirect(voff_t[:]))
 
         part_sum = sb.tile([NQ, 2 * PAGES], F32, name="part_sum")
-        w_bf = sb.tile([P, PAGES, NQ, PACK], BF16, name="w_bf", tag="vsc_then_w", align_bytes=64)
+        w_bf = shared.tile([P, PAGES, NQ, PACK], BF16, name="w_bf", offset=VSC_AT, align_bytes=64)
         for g in range(PAGES):
             prob = sb.tile([NQ, PACK, P], F32, name=f"prob{g}", tag=f"prob{g}", align_bytes=64)
             prob_t = ps.tile([P, PACK, NQ], F32, name=f"prob_t{g}")
@@ -180,7 +182,7 @@ def tile_attend_pkv8_soft_kernel(tc, qT, k_words, k_scales, v_words, v_scales, v
                     stop=(g == PAGES - 1),
                 )
 
-        inv_total = sb.tile([NQ, 1], F32, name="inv_total", tag="vsc_then_w", align_bytes=64)
+        inv_total = shared.tile([NQ, 1], F32, name="inv_total", offset=VSC_AT, align_bytes=64)
         nc.vector.reciprocal(inv_total[:], total[:])
         y0 = sb.tile([NQ, HALF], F32, name="y0")
         nc.vector.tensor_scalar(y0[:], acc[0][:], inv_total[:], None, ALU.mult)

@@ -24,6 +24,8 @@ K_ROW0 = 32
 K_ROW_END = 96
 VS_ROW = P - 1
 HALF = DV // 2
+EXP_PLANES = (((0, 2), (2, 4)), ((0, 2), (2, 3), (3, 4)))
+KEY_PIECES = ((0, 512), (512, 768), (768, 1024))
 VSC_AT = NQ + 4 * P
 KEY_ZERO_SPLIT = 512
 TOKEN_ZERO_SPLIT = 2000
@@ -105,54 +107,47 @@ def tile_attend_pkv8_soft_kernel(tc, qT, k_words, k_scales, v_words, v_scales, v
             nc.scalar.copy(tok_col[:], tok_ps[:, :, VS_ROW])
             tok_cols.append(tok_col)
 
-        scores = []
-        for g in range(PAGES):
-            k_g = sb.tile([P, PAGE], U32, name=f"k_g{g}", align_bytes=64)
-            nc.vector.tensor_copy(
-                k_g[:], k_pool[:].bitcast(U32).indirect(off_t[:, g * PAGE // 16 : (g + 1) * PAGE // 16])
-            )
-            score = ps.tile([NQ, PAGE], F32, name=f"score{g}")
+        scores = [ps.tile([NQ, PAGE], F32, name=f"score{g}") for g in range(PAGES)]
+        for start, end in KEY_PIECES:
+            g, at = divmod(start, PAGE)
+            k_g = sb.tile([P, end - start], U32, name=f"k_g{start}", align_bytes=64)
+            nc.vector.tensor_copy(k_g[:], k_pool[:].bitcast(U32).indirect(off_t[:, start // 16 : end // 16]))
             nc.tensor.matmul_mx(
-                out=score[:],
+                out=scores[g][:, at : at + end - start],
                 lhsT=q_codes[:].bitcast(FP8X4),
                 lhsT_scale=q_sc[:],
                 rhs=k_g[:].bitcast(FP8X4),
-                rhs_scale=ks_plane[:, g * PAGE : (g + 1) * PAGE],
+                rhs_scale=ks_plane[:, start:end],
                 start=True,
                 stop=True,
             )
-            scores.append(score)
 
         neg_first = sb.tile([NQ, 1], F32, name="neg_first")
         neg_max = sb.tile([NQ, 1], F32, name="neg_max")
-        negated0 = sb.tile([NQ, PAGE], F32, name="negated0", tag="neg0_then_vsc", align_bytes=64)
-        nc.vector.tensor_scalar(negated0[:], scores[0][:], -1.0, None, ALU.mult, ALU.min, accum_out=neg_first[:])
-        negated1 = sb.tile([NQ, PAGE], F32, name="negated1", tag="neg1_then_v", align_bytes=64)
+        nc.vector.tensor_reduce(neg_first[:], scores[0][:], mybir.AxisListType.X, ALU.max, negate=True)
+        negated1 = sb.tile([NQ, PAGE], F32, name="negated1", align_bytes=64)
         nc.vector.tensor_scalar(
             negated1[:], scores[1][:], -1.0, neg_first[:], ALU.mult, ALU.min, accum_out=neg_max[:]
         )
-        v_g = sb.tile([P, PAGES * DV], U32, name="v_g", tag="neg0_then_vsc", align_bytes=64)
+        v_g = sb.tile([P, PAGES * DV], U32, name="v_g", align_bytes=64)
         nc.vector.tensor_copy(v_g[:], v_pool[:].bitcast(U32).indirect(voff_t[:]))
-        vsc_g = sb.tile([P, PAGES * DV], U8, name="vsc_g", tag="neg1_then_v", align_bytes=64)
+        vsc_g = sb.tile([P, PAGES * DV], U8, name="vsc_g", align_bytes=64)
         nc.vector.tensor_copy(vsc_g[:], vsc_pool[:].indirect(voff_t[:]))
 
-        part_sum = sb.tile([NQ, 2 * PAGES], F32, name="part_sum")
+        prob = sb.tile([NQ, PAGES, PACK, P], F32, name="prob", tag="prob_then_codes", align_bytes=64)
         w_bf = shared.tile([P, PAGES, NQ, PACK], BF16, name="w_bf", offset=VSC_AT, align_bytes=64)
         for g in range(PAGES):
-            prob = sb.tile([NQ, PACK, P], F32, name=f"prob{g}", tag=f"prob{g}", align_bytes=64)
             prob_t = ps.tile([P, PACK, NQ], F32, name=f"prob_t{g}")
-            for u in range(2):
-                pair = slice(2 * u, 2 * u + 2)
+            for first, end in EXP_PLANES[g]:
                 nc.scalar.activation(
-                    prob[:, pair, :].rearrange("q t s -> q s t"),
-                    scores[g][:].rearrange("q (s t) -> q s t", t=PACK)[:, :, pair],
+                    prob[:, g, first:end, :].rearrange("q t s -> q s t"),
+                    scores[g][:].rearrange("q (s t) -> q s t", t=PACK)[:, :, first:end],
                     ACT.Exp,
                     bias=neg_max[:],
                     scale=1.0,
-                    accum_out=part_sum[:, 2 * g + u : 2 * g + u + 1],
                 )
-                for t in range(2 * u, 2 * u + 2):
-                    nc.tensor.transpose(prob_t[:, t, :], prob[:, t, :], ident[:])
+                for t in range(first, end):
+                    nc.tensor.transpose(prob_t[:, t, :], prob[:, g, t, :], ident[:])
             nc.vector.tensor_tensor(
                 w_bf[:, g],
                 prob_t[:].rearrange("s t q -> s q t"),
@@ -161,12 +156,15 @@ def tile_attend_pkv8_soft_kernel(tc, qT, k_words, k_scales, v_words, v_scales, v
             )
 
         total = sb.tile([NQ, 1], F32, name="total")
-        sum_copy = sb.tile([NQ, 2 * PAGES], F32, name="sum_copy")
-        nc.scalar.activation(sum_copy[:], part_sum[:], ACT.Identity, accum_out=total[:])
+        sum_copy = sb.tile([NQ, N], F32, name="sum_copy")
+        nc.scalar.activation(
+            sum_copy[:], prob[:].rearrange("q g t s -> q (g t s)"), ACT.Identity, accum_out=total[:]
+        )
 
+        code_tags = ["prob_then_codes", "w_codes1"]
         acc = [ps.tile([NQ, HALF], F32, name=f"acc{h}") for h in range(2)]
         for g in range(PAGES):
-            w_codes = sb.tile([P, NQ], U32, name=f"w_codes{g}", tag=f"prob{PAGES - 1 - g}", align_bytes=64)
+            w_codes = sb.tile([P, NQ], U32, name=f"w_codes{g}", tag=code_tags[g], align_bytes=64)
             w_sc = sb.tile([P, NQ], U8, name=f"w_sc{g}", align_bytes=64)
             nc.vector.quantize_mx(
                 out=w_codes[:].bitcast(FP8X4), scales=w_sc[:], in_=w_bf[:, g].rearrange("s q t -> s (q t)")

@@ -60,7 +60,6 @@ def tile_attend_pkv8_soft_kernel(tc, qT, k_words, k_scales, v_words, v_scales, v
         nc.sync.dma_start(ks_pool[:].bitcast(I32)[K_ROW0:K_ROW_END:ROW_STEP, :], k_scales[0].bitcast(I32))
         nc.sync.dma_start(tok_pool[VS_ROW:P, :], vs[0:1, :])
         nc.sync.dma_start(k_pool[:], k_words[0].rearrange("p n t -> p (n t)").bitcast(I32))
-        nc.sync.dma_start(voff_t[:], voffs)
 
         q_bf = sb.tile([P, NQ, PACK], BF16, name="q_bf", align_bytes=64)
         nc.scalar.copy(q_bf[:], q_raw[:].rearrange("p j q -> p q j"))
@@ -76,6 +75,7 @@ def tile_attend_pkv8_soft_kernel(tc, qT, k_words, k_scales, v_words, v_scales, v
                 ks_plane[:].bitcast(I32)[r:P:32, :],
                 ks_g[:].bitcast(I32)[K_ROW0 + ROW_STEP * r : K_ROW_END : 4 * ROW_STEP, :],
             )
+        nc.sync.dma_start(voff_t[:], voffs)
         v_pool = sb.tile([P, POOL_PAGES * DV], I32, name="v_pool", align_bytes=64)
         nc.sync.dma_start(
             v_pool[:].rearrange("p (u e) -> p u e", e=DV),

@@ -182,9 +182,7 @@ def tile_attend_pkv8_soft_kernel(tc, qT, k_words, k_scales, v_words, v_scales, v
 
         inv_total = shared.tile([NQ, 1], F32, name="inv_total", offset=VSC_AT, align_bytes=64)
         nc.vector.reciprocal(inv_total[:], total[:])
-        y0 = sb.tile([NQ, HALF], F32, name="y0")
-        nc.vector.tensor_scalar(y0[:], acc[0][:], inv_total[:], None, ALU.mult)
-        nc.sync.dma_start(out[0][:, 0:HALF], y0[:])
-        y1 = sb.tile([NQ, HALF], F32, name="y1")
-        nc.scalar.activation(y1[:], acc[1][:], ACT.Copy, scale=inv_total[:])
-        nc.scalar.dma_start(out[0][:, HALF:DV], y1[:])
+        y = sb.tile([NQ, DV], F32, name="y")
+        nc.scalar.activation(y[:, 0:HALF], acc[0][:], ACT.Copy, scale=inv_total[:])
+        nc.vector.tensor_scalar(y[:, HALF:DV], acc[1][:], inv_total[:], None, ALU.mult)
+        nc.sync.dma_start(out[0], y[:])

@@ -19,16 +19,15 @@ PAGE = 512
 N, T, D, DV, NQ = 1024, 4096, 512, 256, 128
 PAGES = N // PAGE
 POOL_PAGES = T // PAGE
+LIST_ROWS = 16
+QUADRANT = 32
 ROW_STEP = 4
 K_ROW0 = 32
 K_ROW_END = 96
 VS_ROW = P - 1
 HALF = DV // 2
-EXP_PLANES = (((0, 2), (2, 4)), ((0, 2), (2, 3), (3, 4)))
-KEY_PIECES = ((0, 512), (512, 768), (768, 1024))
-VSC_AT = NQ + 4 * P
-KEY_ZERO_SPLIT = 512
-TOKEN_ZERO_SPLIT = 2000
+KEY_PIECE = 256
+EXP_PLACES = (((0, 2), (2, 4)), ((0, 2), (2, 3), (3, 4)))
 
 FLOPS = 2 * NQ * N * (D + DV)
 
@@ -41,40 +40,39 @@ def tile_attend_pkv8_soft_kernel(tc, qT, k_words, k_scales, v_words, v_scales, v
         shared = ctx.enter_context(tc.tile_pool(name="shared", bufs=1))
         ps = ctx.enter_context(tc.psum_pool(name="ps", bufs=1))
 
-        off_t = lists.tile([P, N // 16], U16, name="off_t")
-        voff_t = lists.tile([P, PAGES * DV // 16], U16, name="voff_t")
+        off_t = lists.tile([P, N // LIST_ROWS], U16, name="off_t")
+        voff_t = lists.tile([P, PAGES * DV // LIST_ROWS], U16, name="voff_t")
         q_raw = sb.tile([P, PACK, NQ], F32, name="q_raw", align_bytes=64)
         ks_pool = shared.tile([P, T], U8, name="ks_pool", offset=0, align_bytes=64)
         tok_pool = sb.tile([P, T], F32, name="tok_pool", align_bytes=64)
         k_pool = sb.tile([P, T], I32, name="k_pool", align_bytes=64)
 
-        nc.gpsimd.memset(ks_pool[:].bitcast(I32)[:, 0:KEY_ZERO_SPLIT], 0)
-        nc.vector.memset(ks_pool[:].bitcast(I32)[:, KEY_ZERO_SPLIT : T // 4 - 1], 0)
-        nc.vector.memset(ks_pool[:].bitcast(I32)[:, T // 4 - 1 : T // 4], 0)
-        nc.gpsimd.memset(tok_pool[0:VS_ROW, 0:TOKEN_ZERO_SPLIT], 0.0)
-        nc.vector.memset(tok_pool[0:VS_ROW, TOKEN_ZERO_SPLIT : T - 1], 0.0)
-        nc.vector.memset(tok_pool[0:VS_ROW, T - 1 : T], 0.0)
+        nc.vector.memset(ks_pool[:].bitcast(I32), 0)
+        ident = sb.tile([P, P], F32, name="ident", tag="ident_then_codes", align_bytes=64)
+        nc.vector.memset(ident[:], 0.0)
+        make_identity(nc, ident[:], nomemset=True)
+        nc.vector.memset(tok_pool[0:VS_ROW, :], 0.0)
 
         nc.sync.dma_start(q_raw[:], qT[0].rearrange("(p j) q -> p j q", j=PACK))
         nc.sync.dma_start(off_t[:], offs)
-        nc.sync.dma_start(ks_pool[:].bitcast(I32)[K_ROW0:K_ROW_END:ROW_STEP, :], k_scales[0].bitcast(I32))
         nc.sync.dma_start(tok_pool[VS_ROW:P, :], vs[0:1, :])
+        nc.sync.dma_start(ks_pool[:].bitcast(I32)[K_ROW0:K_ROW_END:ROW_STEP, :], k_scales[0].bitcast(I32))
         nc.sync.dma_start(k_pool[:], k_words[0].rearrange("p n t -> p (n t)").bitcast(I32))
 
         q_bf = sb.tile([P, NQ, PACK], BF16, name="q_bf", align_bytes=64)
         nc.scalar.copy(q_bf[:], q_raw[:].rearrange("p j q -> p q j"))
+
         ks_g = sb.tile([P, N], U8, name="ks_g", align_bytes=64)
         nc.vector.tensor_copy(ks_g[:], ks_pool[:].indirect(off_t[:]))
-        ident = shared.tile([P, P], F32, name="ident", offset=NQ, align_bytes=64)
-        make_identity(nc, ident[:])
-        vsc_pool = shared.tile([P, POOL_PAGES * DV], U8, name="vsc_pool", offset=VSC_AT, align_bytes=64)
+        vsc_pool = shared.tile([P, POOL_PAGES * DV], U8, name="vsc_pool", offset=NQ, align_bytes=64)
         nc.vector.memset(vsc_pool[:].bitcast(I32), 0)
         ks_plane = sb.tile([P, N], U8, name="ks_plane", align_bytes=64)
         for r in range(4):
             nc.sync.dma_start(
-                ks_plane[:].bitcast(I32)[r:P:32, :],
+                ks_plane[:].bitcast(I32)[r:P:QUADRANT, :],
                 ks_g[:].bitcast(I32)[K_ROW0 + ROW_STEP * r : K_ROW_END : 4 * ROW_STEP, :],
             )
+
         nc.sync.dma_start(voff_t[:], voffs)
         v_pool = sb.tile([P, POOL_PAGES * DV], I32, name="v_pool", align_bytes=64)
         nc.sync.dma_start(
@@ -84,16 +82,20 @@ def tile_attend_pkv8_soft_kernel(tc, qT, k_words, k_scales, v_words, v_scales, v
         vsc_rows = v_scales.bitcast(I32).rearrange("u (a r) e -> r a u e", r=4)
         for r in range(4):
             nc.sync.dma_start(
-                vsc_pool[:].bitcast(I32)[r:P:32, :].rearrange("p (u e) -> p u e", u=POOL_PAGES),
+                vsc_pool[:].bitcast(I32)[r:P:QUADRANT, :].rearrange("p (u e) -> p u e", u=POOL_PAGES),
                 vsc_rows[r],
             )
+
         tok_gs = []
         for g in range(PAGES):
             tok_g = sb.tile([P, PAGE], F32, name=f"tok_g{g}")
             nc.scalar.activation(
-                tok_g[:], tok_pool[:].indirect(off_t[:, g * PAGE // 16 : (g + 1) * PAGE // 16]), ACT.Copy
+                tok_g[:],
+                tok_pool[:].indirect(off_t[:, g * PAGE // LIST_ROWS : (g + 1) * PAGE // LIST_ROWS]),
+                ACT.Copy,
             )
             tok_gs.append(tok_g)
+
         q_codes = sb.tile([P, NQ], U32, name="q_codes", align_bytes=64)
         q_sc = shared.tile([P, NQ], U8, name="q_sc", offset=0, align_bytes=64)
         nc.vector.quantize_mx(out=q_codes[:].bitcast(FP8X4), scales=q_sc[:], in_=q_bf[:].rearrange("p q j -> p (q j)"))
@@ -108,12 +110,15 @@ def tile_attend_pkv8_soft_kernel(tc, qT, k_words, k_scales, v_words, v_scales, v
             tok_cols.append(tok_col)
 
         scores = [ps.tile([NQ, PAGE], F32, name=f"score{g}") for g in range(PAGES)]
-        for start, end in KEY_PIECES:
+        for start in range(0, N, KEY_PIECE):
+            end = start + KEY_PIECE
             g, at = divmod(start, PAGE)
-            k_g = sb.tile([P, end - start], U32, name=f"k_g{start}", align_bytes=64)
-            nc.vector.tensor_copy(k_g[:], k_pool[:].bitcast(U32).indirect(off_t[:, start // 16 : end // 16]))
+            k_g = sb.tile([P, KEY_PIECE], U32, name=f"k_g{start}", align_bytes=64)
+            nc.vector.tensor_copy(
+                k_g[:], k_pool[:].bitcast(U32).indirect(off_t[:, start // LIST_ROWS : end // LIST_ROWS])
+            )
             nc.tensor.matmul_mx(
-                out=scores[g][:, at : at + end - start],
+                out=scores[g][:, at : at + KEY_PIECE],
                 lhsT=q_codes[:].bitcast(FP8X4),
                 lhsT_scale=q_sc[:],
                 rhs=k_g[:].bitcast(FP8X4),
@@ -129,24 +134,25 @@ def tile_attend_pkv8_soft_kernel(tc, qT, k_words, k_scales, v_words, v_scales, v
         nc.vector.tensor_scalar(
             negated1[:], scores[1][:], -1.0, neg_first[:], ALU.mult, ALU.min, accum_out=neg_max[:]
         )
+
         v_g = sb.tile([P, PAGES * DV], U32, name="v_g", align_bytes=64)
         nc.vector.tensor_copy(v_g[:], v_pool[:].bitcast(U32).indirect(voff_t[:]))
         vsc_g = sb.tile([P, PAGES * DV], U8, name="vsc_g", align_bytes=64)
         nc.vector.tensor_copy(vsc_g[:], vsc_pool[:].indirect(voff_t[:]))
 
-        prob = sb.tile([NQ, PAGES, PACK, P], F32, name="prob", tag="prob_then_codes", align_bytes=64)
-        w_bf = shared.tile([P, PAGES, NQ, PACK], BF16, name="w_bf", offset=VSC_AT, align_bytes=64)
+        prob = sb.tile([NQ, PAGES, PACK, P], F32, name="prob", align_bytes=64)
+        w_bf = shared.tile([P, PAGES, NQ, PACK], BF16, name="w_bf", offset=NQ, align_bytes=64)
         for g in range(PAGES):
             prob_t = ps.tile([P, PACK, NQ], F32, name=f"prob_t{g}")
-            for first, end in EXP_PLANES[g]:
+            for first, last in EXP_PLACES[g]:
                 nc.scalar.activation(
-                    prob[:, g, first:end, :].rearrange("q t s -> q s t"),
-                    scores[g][:].rearrange("q (s t) -> q s t", t=PACK)[:, :, first:end],
+                    prob[:, g, first:last, :].rearrange("q t s -> q s t"),
+                    scores[g][:].rearrange("q (s t) -> q s t", t=PACK)[:, :, first:last],
                     ACT.Exp,
                     bias=neg_max[:],
                     scale=1.0,
                 )
-                for t in range(first, end):
+                for t in range(first, last):
                     nc.tensor.transpose(prob_t[:, t, :], prob[:, g, t, :], ident[:])
             nc.vector.tensor_tensor(
                 w_bf[:, g],
@@ -161,18 +167,20 @@ def tile_attend_pkv8_soft_kernel(tc, qT, k_words, k_scales, v_words, v_scales, v
             sum_copy[:], prob[:].rearrange("q g t s -> q (g t s)"), ACT.Identity, accum_out=total[:]
         )
 
-        code_tags = ["prob_then_codes", "w_codes1"]
+        w_codes = [
+            sb.tile([P, NQ], U32, name="w_codes0", tag="ident_then_codes", align_bytes=64),
+            sb.tile([P, NQ], U32, name="w_codes1", align_bytes=64),
+        ]
         acc = [ps.tile([NQ, HALF], F32, name=f"acc{h}") for h in range(2)]
         for g in range(PAGES):
-            w_codes = sb.tile([P, NQ], U32, name=f"w_codes{g}", tag=code_tags[g], align_bytes=64)
             w_sc = sb.tile([P, NQ], U8, name=f"w_sc{g}", align_bytes=64)
             nc.vector.quantize_mx(
-                out=w_codes[:].bitcast(FP8X4), scales=w_sc[:], in_=w_bf[:, g].rearrange("s q t -> s (q t)")
+                out=w_codes[g][:].bitcast(FP8X4), scales=w_sc[:], in_=w_bf[:, g].rearrange("s q t -> s (q t)")
             )
             for h in range(2):
                 nc.tensor.matmul_mx(
                     out=acc[h][:],
-                    lhsT=w_codes[:].bitcast(FP8X4),
+                    lhsT=w_codes[g][:].bitcast(FP8X4),
                     lhsT_scale=w_sc[:],
                     rhs=v_g[:, g * DV + h * HALF : g * DV + (h + 1) * HALF].bitcast(FP8X4),
                     rhs_scale=vsc_g[:, g * DV + h * HALF : g * DV + (h + 1) * HALF],
@@ -180,9 +188,9 @@ def tile_attend_pkv8_soft_kernel(tc, qT, k_words, k_scales, v_words, v_scales, v
                     stop=(g == PAGES - 1),
                 )
 
-        inv_total = shared.tile([NQ, 1], F32, name="inv_total", offset=VSC_AT, align_bytes=64)
+        inv_total = shared.tile([NQ, 1], F32, name="inv_total", offset=NQ, align_bytes=64)
         nc.vector.reciprocal(inv_total[:], total[:])
         y = sb.tile([NQ, DV], F32, name="y")
-        nc.scalar.activation(y[:, 0:HALF], acc[0][:], ACT.Copy, scale=inv_total[:])
-        nc.vector.tensor_scalar(y[:, HALF:DV], acc[1][:], inv_total[:], None, ALU.mult)
+        nc.vector.tensor_scalar(y[:, 0:HALF], acc[0][:], inv_total[:], None, ALU.mult)
+        nc.scalar.activation(y[:, HALF:DV], acc[1][:], ACT.Copy, scale=inv_total[:])
         nc.sync.dma_start(out[0], y[:])

@@ -24,7 +24,8 @@ QUADRANT = 32
 ROW_STEP = 4
 K_ROW0 = 32
 K_ROW_END = 96
-VS_ROW = P - 1
+VS_ROW0 = P - POOL_PAGES
+VECTOR_PAGES = 6
 HALF = DV // 2
 KEY_PIECE = 256
 EXP_PLACES = (((0, 2), (2, 4)), ((0, 2), (2, 3), (3, 4)))
@@ -44,18 +45,21 @@ def tile_attend_pkv8_soft_kernel(tc, qT, k_words, k_scales, v_words, v_scales, v
         voff_t = lists.tile([P, PAGES * DV // LIST_ROWS], U16, name="voff_t")
         q_raw = sb.tile([P, PACK, NQ], F32, name="q_raw", align_bytes=64)
         ks_pool = shared.tile([P, T], U8, name="ks_pool", offset=0, align_bytes=64)
+        vs_rows = sb.tile([P, PAGE], F32, name="vs_rows", align_bytes=64)
         tok_pool = sb.tile([P, T], F32, name="tok_pool", align_bytes=64)
         k_pool = sb.tile([P, T], I32, name="k_pool", align_bytes=64)
 
         nc.vector.memset(ks_pool[:].bitcast(I32), 0)
+        nc.vector.memset(vs_rows[0:VS_ROW0, :], 0.0)
         ident = sb.tile([P, P], F32, name="ident", tag="ident_then_codes", align_bytes=64)
         nc.vector.memset(ident[:], 0.0)
         make_identity(nc, ident[:], nomemset=True)
-        nc.vector.memset(tok_pool[0:VS_ROW, :], 0.0)
+        vsc_pool = shared.tile([P, POOL_PAGES * DV], U8, name="vsc_pool", offset=T, align_bytes=64)
+        nc.vector.memset(vsc_pool[:].bitcast(I32), 0)
 
         nc.sync.dma_start(q_raw[:], qT[0].rearrange("(p j) q -> p j q", j=PACK))
         nc.sync.dma_start(off_t[:], offs)
-        nc.sync.dma_start(tok_pool[VS_ROW:P, :], vs[0:1, :])
+        nc.sync.dma_start(vs_rows[VS_ROW0:P, :], vs[0].rearrange("(u j) -> u j", j=PAGE))
         nc.sync.dma_start(ks_pool[:].bitcast(I32)[K_ROW0:K_ROW_END:ROW_STEP, :], k_scales[0].bitcast(I32))
         nc.sync.dma_start(k_pool[:], k_words[0].rearrange("p n t -> p (n t)").bitcast(I32))
 
@@ -64,8 +68,6 @@ def tile_attend_pkv8_soft_kernel(tc, qT, k_words, k_scales, v_words, v_scales, v
 
         ks_g = sb.tile([P, N], U8, name="ks_g", align_bytes=64)
         nc.vector.tensor_copy(ks_g[:], ks_pool[:].indirect(off_t[:]))
-        vsc_pool = shared.tile([P, POOL_PAGES * DV], U8, name="vsc_pool", offset=NQ, align_bytes=64)
-        nc.vector.memset(vsc_pool[:].bitcast(I32), 0)
         ks_plane = sb.tile([P, N], U8, name="ks_plane", align_bytes=64)
         for r in range(4):
             nc.sync.dma_start(
@@ -86,6 +88,23 @@ def tile_attend_pkv8_soft_kernel(tc, qT, k_words, k_scales, v_words, v_scales, v
                 vsc_rows[r],
             )
 
+        vs_ps = ps.tile([P, PACK, P], F32, name="vs_ps")
+        for t in range(PACK):
+            nc.tensor.transpose(vs_ps[:, t, :], vs_rows[:, t:PAGE:PACK], ident[:])
+        vs_cols = sb.tile([P, POOL_PAGES, PACK], F32, name="vs_cols", align_bytes=64)
+        nc.scalar.copy(vs_cols[:], vs_ps[:, :, VS_ROW0:P].rearrange("s t u -> s u t"))
+        tok_view = tok_pool[:].rearrange("s (u q t) -> s u q t", u=POOL_PAGES, t=PACK)
+        nc.vector.tensor_copy(
+            tok_view[:, 0:VECTOR_PAGES],
+            vs_cols[:, 0:VECTOR_PAGES, :].unsqueeze(2).to_broadcast([P, VECTOR_PAGES, NQ, PACK]),
+        )
+        nc.scalar.copy(
+            tok_view[:, VECTOR_PAGES:POOL_PAGES],
+            vs_cols[:, VECTOR_PAGES:POOL_PAGES, :]
+            .unsqueeze(2)
+            .to_broadcast([P, POOL_PAGES - VECTOR_PAGES, NQ, PACK]),
+        )
+
         tok_gs = []
         for g in range(PAGES):
             tok_g = sb.tile([P, PAGE], F32, name=f"tok_g{g}")
@@ -99,15 +118,6 @@ def tile_attend_pkv8_soft_kernel(tc, qT, k_words, k_scales, v_words, v_scales, v
         q_codes = sb.tile([P, NQ], U32, name="q_codes", align_bytes=64)
         q_sc = shared.tile([P, NQ], U8, name="q_sc", offset=0, align_bytes=64)
         nc.vector.quantize_mx(out=q_codes[:].bitcast(FP8X4), scales=q_sc[:], in_=q_bf[:].rearrange("p q j -> p (q j)"))
-
-        tok_cols = []
-        for g in range(PAGES):
-            tok_ps = ps.tile([P, PACK, P], F32, name=f"tok_ps{g}")
-            for t in range(PACK):
-                nc.tensor.transpose(tok_ps[:, t, :], tok_gs[g][:, t:PAGE:PACK], ident[:])
-            tok_col = sb.tile([P, PACK], F32, name=f"tok_col{g}", align_bytes=64)
-            nc.scalar.copy(tok_col[:], tok_ps[:, :, VS_ROW])
-            tok_cols.append(tok_col)
 
         scores = [ps.tile([NQ, PAGE], F32, name=f"score{g}") for g in range(PAGES)]
         for start in range(0, N, KEY_PIECE):
@@ -141,7 +151,7 @@ def tile_attend_pkv8_soft_kernel(tc, qT, k_words, k_scales, v_words, v_scales, v
         nc.vector.tensor_copy(vsc_g[:], vsc_pool[:].indirect(voff_t[:]))
 
         prob = sb.tile([NQ, PAGES, PACK, P], F32, name="prob", align_bytes=64)
-        w_bf = shared.tile([P, PAGES, NQ, PACK], BF16, name="w_bf", offset=NQ, align_bytes=64)
+        w_bf = shared.tile([P, PAGES, NQ, PACK], BF16, name="w_bf", offset=T, align_bytes=64)
         for g in range(PAGES):
             prob_t = ps.tile([P, PACK, NQ], F32, name=f"prob_t{g}")
             for first, last in EXP_PLACES[g]:
@@ -157,7 +167,7 @@ def tile_attend_pkv8_soft_kernel(tc, qT, k_words, k_scales, v_words, v_scales, v
             nc.vector.tensor_tensor(
                 w_bf[:, g],
                 prob_t[:].rearrange("s t q -> s q t"),
-                tok_cols[g][:].unsqueeze(1).to_broadcast([P, NQ, PACK]),
+                tok_gs[g][:].rearrange("s (q t) -> s q t", t=PACK),
                 ALU.mult,
             )
 
@@ -188,7 +198,7 @@ def tile_attend_pkv8_soft_kernel(tc, qT, k_words, k_scales, v_words, v_scales, v
                     stop=(g == PAGES - 1),
                 )
 
-        inv_total = shared.tile([NQ, 1], F32, name="inv_total", offset=NQ, align_bytes=64)
+        inv_total = shared.tile([NQ, 1], F32, name="inv_total", offset=T, align_bytes=64)
         nc.vector.reciprocal(inv_total[:], total[:])
         y = sb.tile([NQ, DV], F32, name="y")
         nc.vector.tensor_scalar(y[:, 0:HALF], acc[0][:], inv_total[:], None, ALU.mult)

@@ -25,7 +25,7 @@ ROW_STEP = 4
 K_ROW0 = 32
 K_ROW_END = 96
 VS_ROW0 = P - POOL_PAGES
-VECTOR_PAGES = 6
+VECTOR_PAGES = 4
 HALF = DV // 2
 KEY_PIECE = 256
 EXP_PLACES = (((0, 2), (2, 4)), ((0, 2), (2, 3), (3, 4)))

@@ -70,7 +70,8 @@ def tile_attend_pkv8_soft_kernel(tc, qT, k_words, k_scales, v_words, v_scales, v
         nc.vector.tensor_copy(ks_g[:], ks_pool[:].indirect(off_t[:]))
         ks_plane = sb.tile([P, N], U8, name="ks_plane", align_bytes=64)
         for r in range(4):
-            nc.sync.dma_start(
+            queue = nc.sync if r < 2 else nc.scalar
+            queue.dma_start(
                 ks_plane[:].bitcast(I32)[r:P:QUADRANT, :],
                 ks_g[:].bitcast(I32)[K_ROW0 + ROW_STEP * r : K_ROW_END : 4 * ROW_STEP, :],
             )
@@ -91,18 +92,18 @@ def tile_attend_pkv8_soft_kernel(tc, qT, k_words, k_scales, v_words, v_scales, v
         vs_ps = ps.tile([P, PACK, P], F32, name="vs_ps")
         for t in range(PACK):
             nc.tensor.transpose(vs_ps[:, t, :], vs_rows[:, t:PAGE:PACK], ident[:])
-        vs_cols = sb.tile([P, POOL_PAGES, PACK], F32, name="vs_cols", align_bytes=64)
-        nc.scalar.copy(vs_cols[:], vs_ps[:, :, VS_ROW0:P].rearrange("s t u -> s u t"))
+        vs_turned = vs_ps[:, :, VS_ROW0:P].rearrange("s t u -> s u t")
+        scalar_pages = POOL_PAGES - VECTOR_PAGES
+        cols_v = sb.tile([P, VECTOR_PAGES, PACK], F32, name="cols_v", align_bytes=64)
+        cols_s = shared.tile([P, scalar_pages, PACK], F32, name="cols_s", offset=NQ, align_bytes=64)
+        nc.vector.tensor_copy(cols_v[:], vs_turned[:, 0:VECTOR_PAGES, :])
+        nc.scalar.copy(cols_s[:], vs_turned[:, VECTOR_PAGES:POOL_PAGES, :])
         tok_view = tok_pool[:].rearrange("s (u q t) -> s u q t", u=POOL_PAGES, t=PACK)
         nc.vector.tensor_copy(
-            tok_view[:, 0:VECTOR_PAGES],
-            vs_cols[:, 0:VECTOR_PAGES, :].unsqueeze(2).to_broadcast([P, VECTOR_PAGES, NQ, PACK]),
+            tok_view[:, 0:VECTOR_PAGES], cols_v[:].unsqueeze(2).to_broadcast([P, VECTOR_PAGES, NQ, PACK])
         )
         nc.scalar.copy(
-            tok_view[:, VECTOR_PAGES:POOL_PAGES],
-            vs_cols[:, VECTOR_PAGES:POOL_PAGES, :]
-            .unsqueeze(2)
-            .to_broadcast([P, POOL_PAGES - VECTOR_PAGES, NQ, PACK]),
+            tok_view[:, VECTOR_PAGES:POOL_PAGES], cols_s[:].unsqueeze(2).to_broadcast([P, scalar_pages, NQ, PACK])
         )
 
         tok_gs = []

from contextlib import ExitStack

import concourse.mybir as mybir
from concourse.masks import make_identity

F32 = mybir.dt.float32
BF16 = mybir.dt.bfloat16
I32 = mybir.dt.int32
U32 = mybir.dt.uint32
U16 = mybir.dt.uint16
U8 = mybir.dt.uint8
FP8X4 = mybir.dt.float8_e4m3fn_x4
ALU = mybir.AluOpType
ACT = mybir.ActivationFunctionType

P = 128
PACK = 4
PAGE = 512
N, T, D, DV, NQ = 1024, 4096, 512, 256, 128
PAGES = N // PAGE
POOL_PAGES = T // PAGE
LIST_ROWS = 16
QUADRANT = 32
ROW_STEP = 4
K_ROW0 = 32
K_ROW_END = 96
VS_ROW0 = P - POOL_PAGES
VECTOR_PAGES = 4
HALF = DV // 2
KEY_PIECE = 256
EXP_PLACES = (((0, 2), (2, 4)), ((0, 2), (2, 3), (3, 4)))

FLOPS = 2 * NQ * N * (D + DV)


def tile_attend_pkv8_soft_kernel(tc, qT, k_words, k_scales, v_words, v_scales, vs, offs, voffs, out):
    nc = tc.nc
    with ExitStack() as ctx:
        lists = ctx.enter_context(tc.tile_pool(name="lists", bufs=1))
        sb = ctx.enter_context(tc.tile_pool(name="sb", bufs=1))
        shared = ctx.enter_context(tc.tile_pool(name="shared", bufs=1))
        ps = ctx.enter_context(tc.psum_pool(name="ps", bufs=1))

        off_t = lists.tile([P, N // LIST_ROWS], U16, name="off_t")
        voff_t = lists.tile([P, PAGES * DV // LIST_ROWS], U16, name="voff_t")
        q_raw = sb.tile([P, PACK, NQ], F32, name="q_raw", align_bytes=64)
        ks_pool = shared.tile([P, T], U8, name="ks_pool", offset=0, align_bytes=64)
        vs_rows = sb.tile([P, PAGE], F32, name="vs_rows", align_bytes=64)
        tok_pool = sb.tile([P, T], F32, name="tok_pool", align_bytes=64)
        k_pool = sb.tile([P, T], I32, name="k_pool", align_bytes=64)

        nc.vector.memset(ks_pool[:].bitcast(I32), 0)
        nc.vector.memset(vs_rows[0:VS_ROW0, :], 0.0)
        ident = sb.tile([P, P], F32, name="ident", tag="ident_then_codes", align_bytes=64)
        nc.vector.memset(ident[:], 0.0)
        make_identity(nc, ident[:], nomemset=True)
        vsc_pool = shared.tile([P, POOL_PAGES * DV], U8, name="vsc_pool", offset=T, align_bytes=64)
        nc.vector.memset(vsc_pool[:].bitcast(I32), 0)

        nc.sync.dma_start(q_raw[:], qT[0].rearrange("(p j) q -> p j q", j=PACK))
        nc.sync.dma_start(off_t[:], offs)
        nc.sync.dma_start(vs_rows[VS_ROW0:P, :], vs[0].rearrange("(u j) -> u j", j=PAGE))
        nc.sync.dma_start(ks_pool[:].bitcast(I32)[K_ROW0:K_ROW_END:ROW_STEP, :], k_scales[0].bitcast(I32))
        nc.sync.dma_start(k_pool[:], k_words[0].rearrange("p n t -> p (n t)").bitcast(I32))

        q_bf = sb.tile([P, NQ, PACK], BF16, name="q_bf", align_bytes=64)
        nc.scalar.copy(q_bf[:], q_raw[:].rearrange("p j q -> p q j"))

        ks_g = sb.tile([P, N], U8, name="ks_g", align_bytes=64)
        nc.vector.tensor_copy(ks_g[:], ks_pool[:].indirect(off_t[:]))
        ks_plane = sb.tile([P, N], U8, name="ks_plane", align_bytes=64)
        for r in range(4):
            queue = nc.sync if r < 2 else nc.scalar
            queue.dma_start(
                ks_plane[:].bitcast(I32)[r:P:QUADRANT, :],
                ks_g[:].bitcast(I32)[K_ROW0 + ROW_STEP * r : K_ROW_END : 4 * ROW_STEP, :],
            )

        nc.sync.dma_start(voff_t[:], voffs)
        v_pool = sb.tile([P, POOL_PAGES * DV], I32, name="v_pool", align_bytes=64)
        nc.sync.dma_start(
            v_pool[:].rearrange("p (u e) -> p u e", e=DV),
            v_words.rearrange("u p e t -> p u (e t)").bitcast(I32),
        )
        vsc_rows = v_scales.bitcast(I32).rearrange("u (a r) e -> r a u e", r=4)
        for r in range(4):
            nc.sync.dma_start(
                vsc_pool[:].bitcast(I32)[r:P:QUADRANT, :].rearrange("p (u e) -> p u e", u=POOL_PAGES),
                vsc_rows[r],
            )

        vs_ps = ps.tile([P, PACK, P], F32, name="vs_ps")
        for t in range(PACK):
            nc.tensor.transpose(vs_ps[:, t, :], vs_rows[:, t:PAGE:PACK], ident[:])
        vs_turned = vs_ps[:, :, VS_ROW0:P].rearrange("s t u -> s u t")
        scalar_pages = POOL_PAGES - VECTOR_PAGES
        cols_v = sb.tile([P, VECTOR_PAGES, PACK], F32, name="cols_v", align_bytes=64)
        cols_s = shared.tile([P, scalar_pages, PACK], F32, name="cols_s", offset=NQ, align_bytes=64)
        nc.vector.tensor_copy(cols_v[:], vs_turned[:, 0:VECTOR_PAGES, :])
        nc.scalar.copy(cols_s[:], vs_turned[:, VECTOR_PAGES:POOL_PAGES, :])
        tok_view = tok_pool[:].rearrange("s (u q t) -> s u q t", u=POOL_PAGES, t=PACK)
        nc.vector.tensor_copy(
            tok_view[:, 0:VECTOR_PAGES], cols_v[:].unsqueeze(2).to_broadcast([P, VECTOR_PAGES, NQ, PACK])
        )
        nc.scalar.copy(
            tok_view[:, VECTOR_PAGES:POOL_PAGES], cols_s[:].unsqueeze(2).to_broadcast([P, scalar_pages, NQ, PACK])
        )

        tok_gs = []
        for g in range(PAGES):
            tok_g = sb.tile([P, PAGE], F32, name=f"tok_g{g}")
            nc.scalar.activation(
                tok_g[:],
                tok_pool[:].indirect(off_t[:, g * PAGE // LIST_ROWS : (g + 1) * PAGE // LIST_ROWS]),
                ACT.Copy,
            )
            tok_gs.append(tok_g)

        q_codes = sb.tile([P, NQ], U32, name="q_codes", align_bytes=64)
        q_sc = shared.tile([P, NQ], U8, name="q_sc", offset=0, align_bytes=64)
        nc.vector.quantize_mx(out=q_codes[:].bitcast(FP8X4), scales=q_sc[:], in_=q_bf[:].rearrange("p q j -> p (q j)"))

        scores = [ps.tile([NQ, PAGE], F32, name=f"score{g}") for g in range(PAGES)]
        for start in range(0, N, KEY_PIECE):
            end = start + KEY_PIECE
            g, at = divmod(start, PAGE)
            k_g = sb.tile([P, KEY_PIECE], U32, name=f"k_g{start}", align_bytes=64)
            nc.vector.tensor_copy(
                k_g[:], k_pool[:].bitcast(U32).indirect(off_t[:, start // LIST_ROWS : end // LIST_ROWS])
            )
            nc.tensor.matmul_mx(
                out=scores[g][:, at : at + KEY_PIECE],
                lhsT=q_codes[:].bitcast(FP8X4),
                lhsT_scale=q_sc[:],
                rhs=k_g[:].bitcast(FP8X4),
                rhs_scale=ks_plane[:, start:end],
                start=True,
                stop=True,
            )

        neg_first = sb.tile([NQ, 1], F32, name="neg_first")
        neg_max = sb.tile([NQ, 1], F32, name="neg_max")
        nc.vector.tensor_reduce(neg_first[:], scores[0][:], mybir.AxisListType.X, ALU.max, negate=True)
        negated1 = sb.tile([NQ, PAGE], F32, name="negated1", align_bytes=64)
        nc.vector.tensor_scalar(
            negated1[:], scores[1][:], -1.0, neg_first[:], ALU.mult, ALU.min, accum_out=neg_max[:]
        )

        v_g = sb.tile([P, PAGES * DV], U32, name="v_g", align_bytes=64)
        nc.vector.tensor_copy(v_g[:], v_pool[:].bitcast(U32).indirect(voff_t[:]))
        vsc_g = sb.tile([P, PAGES * DV], U8, name="vsc_g", align_bytes=64)
        nc.vector.tensor_copy(vsc_g[:], vsc_pool[:].indirect(voff_t[:]))

        prob = sb.tile([NQ, PAGES, PACK, P], F32, name="prob", align_bytes=64)
        w_bf = shared.tile([P, PAGES, NQ, PACK], BF16, name="w_bf", offset=T, align_bytes=64)
        for g in range(PAGES):
            prob_t = ps.tile([P, PACK, NQ], F32, name=f"prob_t{g}")
            for first, last in EXP_PLACES[g]:
                nc.scalar.activation(
                    prob[:, g, first:last, :].rearrange("q t s -> q s t"),
                    scores[g][:].rearrange("q (s t) -> q s t", t=PACK)[:, :, first:last],
                    ACT.Exp,
                    bias=neg_max[:],
                    scale=1.0,
                )
                for t in range(first, last):
                    nc.tensor.transpose(prob_t[:, t, :], prob[:, g, t, :], ident[:])
            nc.vector.tensor_tensor(
                w_bf[:, g],
                prob_t[:].rearrange("s t q -> s q t"),
                tok_gs[g][:].rearrange("s (q t) -> s q t", t=PACK),
                ALU.mult,
            )

        total = sb.tile([NQ, 1], F32, name="total")
        sum_copy = sb.tile([NQ, N], F32, name="sum_copy")
        nc.scalar.activation(
            sum_copy[:], prob[:].rearrange("q g t s -> q (g t s)"), ACT.Identity, accum_out=total[:]
        )

        w_codes = [
            sb.tile([P, NQ], U32, name="w_codes0", tag="ident_then_codes", align_bytes=64),
            sb.tile([P, NQ], U32, name="w_codes1", align_bytes=64),
        ]
        acc = [ps.tile([NQ, HALF], F32, name=f"acc{h}") for h in range(2)]
        for g in range(PAGES):
            w_sc = sb.tile([P, NQ], U8, name=f"w_sc{g}", align_bytes=64)
            nc.vector.quantize_mx(
                out=w_codes[g][:].bitcast(FP8X4), scales=w_sc[:], in_=w_bf[:, g].rearrange("s q t -> s (q t)")
            )
            for h in range(2):
                nc.tensor.matmul_mx(
                    out=acc[h][:],
                    lhsT=w_codes[g][:].bitcast(FP8X4),
                    lhsT_scale=w_sc[:],
                    rhs=v_g[:, g * DV + h * HALF : g * DV + (h + 1) * HALF].bitcast(FP8X4),
                    rhs_scale=vsc_g[:, g * DV + h * HALF : g * DV + (h + 1) * HALF],
                    start=(g == 0),
                    stop=(g == PAGES - 1),
                )

        inv_total = shared.tile([NQ, 1], F32, name="inv_total", offset=T, align_bytes=64)
        nc.vector.reciprocal(inv_total[:], total[:])
        y = sb.tile([NQ, DV], F32, name="y")
        nc.vector.tensor_scalar(y[:, 0:HALF], acc[0][:], inv_total[:], None, ALU.mult)
        nc.scalar.activation(y[:, HALF:DV], acc[1][:], ACT.Copy, scale=inv_total[:])
        nc.sync.dma_start(out[0], y[:])
